import numpy as np
import ml_dtypes


def mxq(x, axis, fmt="e4m3"):
    dtype, down = {"e4m3": (ml_dtypes.float8_e4m3fn, 7), "e5m2": (ml_dtypes.float8_e5m2, 14)}[fmt]
    v = np.moveaxis(np.asarray(x, np.float32).astype(ml_dtypes.bfloat16).astype(np.float64), axis, -1)
    blocks = v.reshape(v.shape[:-1] + (-1, 32))
    amax = np.abs(blocks).max(-1, keepdims=True)
    byte = np.maximum(np.where(amax > 0, np.frexp(amax)[1] - 1 + 127, 0) - down, 1)
    scale = np.exp2(byte - 127.0)
    codes = (blocks / scale).astype(np.float32).astype(dtype).astype(np.float64)
    return np.moveaxis((codes * scale).reshape(v.shape), -1, axis)


WIDE = False


def mx_kscale(k):
    if not WIDE:
        return np.ones(k)
    levels = np.array([10, -10, 5, -5, 0])
    if k % 512:
        return np.exp2(np.random.permutation(np.resize(levels, k // 32))).repeat(32)
    a = np.empty((k // 512, 16))
    for p in range(k // 512):
        a[p, :8] = np.random.permutation(np.resize(levels, 8))
        for g in range(8):
            far = levels[np.abs(levels - a[p, g]) >= 10]
            a[p, g + 8] = far[np.random.randint(len(far))]
    return np.exp2(a.ravel()).repeat(32)


BF16 = ml_dtypes.bfloat16


def bf(x):
    return np.asarray(x, np.float32).astype(BF16)


def f64(x):
    return np.asarray(x).astype(np.float64)


E2M1 = np.array([0.0, 0.5, 1.0, 1.5, 2.0, 3.0, 4.0, 6.0, -0.0, -0.5, -1.0, -1.5, -2.0, -3.0, -4.0, -6.0])


def pack_weight(w, fmt):
    k, n = w.shape
    w = f64(bf(w)).reshape(k // 32, 32, n)
    amax = np.abs(w).max(1)
    if fmt == "e4m3":
        byte = np.frexp(amax)[1] - 1 + 127 - 7
    else:
        mant, ex = np.frexp(amax / 6.0)
        byte = np.where(mant > 0.5, ex, ex - 1) + 127
    byte = np.clip(np.where(amax > 0, byte, 1), 1, 254)
    scaled = (w * np.exp2(127.0 - byte)[:, None, :]).reshape(k, n).astype(np.float32)
    by_word = np.ascontiguousarray(scaled.reshape(k // 512, 128, 4, n).transpose(0, 1, 3, 2))
    if fmt == "e4m3":
        words = by_word.astype(ml_dtypes.float8_e4m3fn).view(np.uint8)
    else:
        c = by_word.astype(ml_dtypes.float4_e2m1fn).view(np.uint8) & 0xF
        words = c[..., 0::2] | (c[..., 1::2] << 4)
    return np.ascontiguousarray(words), np.ascontiguousarray(byte.astype(np.uint8).reshape(k // 512, 16, n))


def unpack_weight(words, scales, fmt):
    g, p, n, _ = words.shape
    if fmt == "e4m3":
        vals = np.ascontiguousarray(words).view(ml_dtypes.float8_e4m3fn).astype(np.float64)
    else:
        nib = np.empty((g, p, n, 4), np.uint8)
        nib[..., 0::2] = words & 0xF
        nib[..., 1::2] = words >> 4
        vals = E2M1[nib]
    vals = vals * np.repeat(np.exp2(scales.astype(np.float64) - 127.0), 8, axis=1)[..., None]
    return vals.transpose(0, 1, 3, 2).reshape(g * 512, n)
def pack4(w):
    words, scales = pack_weight(w, "e2m1")
    return words.reshape(words.shape[0], 128, -1), scales


def unpack4(words, scales):
    return unpack_weight(words.reshape(words.shape[0], 128, -1, 2), scales, "e2m1")


def planes(Y):
    n, m = Y.shape
    b = f64(bf(Y)).reshape(n // 32, 32, m)
    amax = np.abs(b).max(1)
    byte = np.clip(np.where(amax > 0, np.frexp(amax)[1] - 1 + 127 - 7, 1), 1, 254)
    codes = (b * np.exp2(127.0 - byte)[:, None, :]).reshape(n, m).astype(np.float32).astype(ml_dtypes.float8_e4m3fn).view(np.uint8)
    words = codes.reshape(n // 512, 128, 4, m).transpose(0, 1, 3, 2)
    return np.ascontiguousarray(words), np.ascontiguousarray(byte.astype(np.uint8).reshape(n // 512, 16, m))


IMG, HT, WD, CS, CD, N, GRP = 4, 16, 16, 512, 1024, 3072, 32
M = IMG * HT * WD
CAP = 6.0


def setup_inputs():
    s1 = mx_kscale(CS)
    s2 = mx_kscale(CD)
    skip = np.random.randn(IMG, HT, WD, CS) * s1
    deep = np.random.randn(IMG, HT, WD, CD) * s2
    w_skip = np.random.randn(CS, N) / np.sqrt(CS + CD) / s1[:, None]
    w_deep = np.random.randn(CD, N) / np.sqrt(CS + CD) / s2[:, None]
    w_deep_words, w_deep_scales = pack4(w_deep)
    spread = 0.8 * np.repeat(np.random.randn(N // GRP), GRP) + 0.3 * np.random.randn(N)
    scale = 0.8 * np.exp(spread)
    shift = scale * (1.5 + 0.3 * np.random.randn(N))
    return {"skip": bf(skip), "deep": bf(deep), "w_skip": bf(w_skip),
            "w_deep_words": w_deep_words, "w_deep_scales": w_deep_scales,
            "scale": bf(scale), "shift": bf(shift)}


def reference(skip, deep, w_skip, w_deep_words, w_deep_scales, scale, shift):
    xs = mxq(f64(skip).reshape(M, CS), 1, "e4m3")
    xd = mxq(f64(deep).reshape(M, CD), 1, "e4m3")
    ws = mxq(f64(w_skip), 0, "e4m3")
    wd = unpack4(w_deep_words, w_deep_scales)
    h = (xs @ ws) + (xd @ wd)
    z = h * f64(scale) + f64(shift)
    y = np.minimum(np.maximum(z, 0.0), CAP).reshape(IMG, HT, WD, N)
    Y = y.reshape(M, N).T
    words, scales = planes(Y)
    return y, words, scales

@@ -1,0 +1,399 @@
+from contextlib import ExitStack
+
+import concourse.mybir as mybir
+from concourse.masks import make_identity
+
+F32 = mybir.dt.float32
+BF16 = mybir.dt.bfloat16
+U32 = mybir.dt.uint32
+I32 = mybir.dt.int32
+U8 = mybir.dt.uint8
+FP8X4 = mybir.dt.float8_e4m3fn_x4
+FP4X4 = mybir.dt.float4_e2m1fn_x4
+ALU = mybir.AluOpType
+ACT = mybir.ActivationFunctionType
+
+PIXELS, C_SKIP, C_DEEP, C_OUT = 1024, 512, 1024, 3072
+FLOPS = 2 * PIXELS * (C_SKIP + C_DEEP) * C_OUT
+P = 128
+W = 512
+GROUPS = C_OUT // W
+HALVES = PIXELS // W
+PASSES = 3
+CAP = 6.0
+N_ACT = 2
+TRICK = True
+K = 3
+KLAST = 2
+POOL = 0
+
+
+def tile_skip_expand_relu6_g5_kernel(
+    tc, skip, deep, w_skip, w_deep_words, w_deep_scales, scale, shift, out_0, out_1, out_2
+):
+    nc = tc.nc
+    x_skip = skip.flatten_outer_dims()
+    x_deep = deep.flatten_outer_dims()
+    y_hbm = out_0.flatten_outer_dims()
+
+    with ExitStack() as ctx:
+        keep = ctx.enter_context(tc.tile_pool(name="keep", bufs=1))
+        stage = ctx.enter_context(tc.tile_pool(name="stage", bufs=2))
+        deep3 = ctx.enter_context(tc.tile_pool(name="deep3", bufs=3))
+        acc_pool = ctx.enter_context(tc.psum_pool(name="acc", bufs=1))
+        turn_pool = ctx.enter_context(tc.psum_pool(name="turn", bufs=4))
+        ctx.enter_context(tc.manual_schedule())
+
+        ident = keep.tile([P, P], F32, name="ident")
+        vec_rows = keep.tile([P, W], BF16, name="vec_rows")
+        affine = keep.tile([P, 16, 4], F32, name="affine")
+        x_raw = {}
+        for h in range(HALVES):
+            for c in range(PASSES):
+                x_raw[h, c] = keep.tile([P, 4, W], BF16, name="x_raw_%d_%d" % (h, c))
+        x_codes = keep.tile([P, PASSES, PIXELS], U32, name="x_codes", align_bytes=64)
+        x_scales = keep.tile([P, PASSES, PIXELS], U8, name="x_scales", align_bytes=64)
+        ws_raw, wd_raw, wd_words, wd_scales = {}, {}, {}, {}
+        for g in range(GROUPS):
+            wd_words[g] = keep.tile([P, 2, 2 * W], U8, name="wd_words_%d" % g, align_bytes=64)
+            wd_scales[g] = keep.tile([P, 2, W], U8, name="wd_scales_%d" % g, align_bytes=64)
+        ws_codes = keep.tile([P, GROUPS, W], U32, name="ws_codes", align_bytes=64)
+        ws_scales = keep.tile([P, GROUPS, W], U8, name="ws_scales", align_bytes=64)
+        sraw_first = keep.tile([P, 2, 2 * W], U8, name="sraw_first")
+        sraw_rest = keep.tile([P, 2, C_OUT - 2 * W], U8, name="sraw_rest")
+
+        x_grouped, ws_grouped, acc, act_out, banks, y_out, y_bf, y_codes, y_scales = {}, {}, {}, {}, {}, {}, {}, {}, {}
+
+        def load_x(h, c, pieces):
+            rows = slice(h * W, (h + 1) * W)
+            src = x_skip[rows, :] if c == 0 else x_deep[rows, (c - 1) * W : c * W]
+            src = src.rearrange("(b p i) k -> p b i k", p=P, i=2)
+            dst = x_raw[h, c][:].rearrange("p (b i) k -> p b i k", i=2)
+            if pieces == 2:
+                for b in range(2):
+                    nc.sync.dma_start(out=dst[:, b, :, :], in_=src[:, b, :, :])
+            elif c == 0:
+                nc.sync.dma_start(out=dst.rearrange("p b i k -> p b (i k)"), in_=src.rearrange("p b i k -> p b (i k)"))
+            else:
+                for b in range(2):
+                    nc.sync.dma_start(out=dst[:, b, :, :], in_=src[:, b, :, :])
+
+        def load_ws(g, n):
+            cols = slice(g * W, (g + n) * W)
+            raw = keep.tile([P, 4, n * W], BF16, name="ws_raw_%d" % g)
+            nc.sync.dma_start(out=raw[:], in_=w_skip[:, cols].rearrange("(p j) n -> p j n", j=4))
+            for j in range(n):
+                ws_raw[g + j] = raw[:, :, j * W : (j + 1) * W]
+
+        def load_wd(g, n):
+            cols = slice(2 * g * W, 2 * (g + n) * W)
+            src = w_deep_words[:, :, cols].rearrange("c p b -> p c b")
+            raw = keep.tile([P, 2, 2 * n * W], U8, name="wd_raw_%d" % g)
+            nc.sync.dma_start(out=raw[:].bitcast(I32), in_=src.bitcast(I32))
+            for j in range(n):
+                wd_raw[g + j] = raw[:, :, 2 * j * W : 2 * (j + 1) * W]
+
+        def load_scale_rows(tile, cols):
+            for q in range(4):
+                src = w_deep_scales[:, 4 * q : 4 * q + 4, cols].rearrange("c r n -> r c n")
+                nc.sync.dma_start(out=tile[32 * q : 32 * q + 4, :, :].bitcast(I32), in_=src.bitcast(I32))
+
+        def turn_x(h, c, b):
+            bank = turn_pool.tile([P, W], F32, name="bank", tag="bank")
+            banks["x", h, c, b] = bank
+            for i in range(2):
+                words = x_raw[h, c][:, 2 * b + i, :].bitcast(F32)
+                for u in range(2):
+                    j = 2 * i + u
+                    nc.tensor.transpose(bank[:, j * P : (j + 1) * P], words[:, u : 2 * P : 2], ident[:])
+
+        def copy_x(h, c, b, on_vector):
+            if b == 0:
+                x_grouped[h, c] = stage.tile([P, 4 * W], BF16, name="x_grouped", tag="x_grouped", align_bytes=64)
+            dst = x_grouped[h, c][:, b * 2 * W : (b + 1) * 2 * W].bitcast(F32).rearrange("p (r j) -> p r j", j=4)
+            src = banks["x", h, c, b][:].rearrange("p (j r) -> p r j", j=4)
+            if on_vector:
+                nc.vector.tensor_copy(out=dst, in_=src)
+            elif (h, c, b) == (0, 0, 0):
+                nc.scalar.activation(
+                    out=x_grouped[h, c][:, 0 : 2 * W].rearrange("p (r j e) -> p r j e", j=4, e=2),
+                    in_=banks["x", h, c, b][:].bitcast(BF16).rearrange("p (j r e) -> p r j e", j=4, e=2),
+                    func=ACT.Copy,
+                )
+            else:
+                nc.scalar.copy(out=dst, in_=src)
+
+        def quantize_x(h, c, b0=0, n=2):
+            cols = slice(h * W + b0 * 2 * P, h * W + (b0 + n) * 2 * P)
+            nc.vector.quantize_mx(
+                out=x_codes[:, c, cols].bitcast(FP8X4), scales=x_scales[:, c, cols],
+                in_=x_grouped[h, c][:, b0 * 2 * W : (b0 + n) * 2 * W],
+            )
+
+        def group_ws(g, t, n, on_vector):
+            if t == 0:
+                ws_grouped[g] = stage.tile([P, 4 * W], BF16, name="ws_grouped", tag="ws_grouped", align_bytes=64)
+            dst = ws_grouped[g][:].rearrange("p (t m j) -> p t m j", t=4, j=4)[:, t : t + n, :, :]
+            src = ws_raw[g].rearrange("p j (m t) -> p t m j", t=4)[:, t : t + n, :, :]
+            if on_vector:
+                nc.vector.tensor_copy(out=dst, in_=src)
+            else:
+                nc.scalar.copy(out=dst, in_=src)
+
+        def quantize_ws(g):
+            nc.vector.quantize_mx(out=ws_codes[:, g, :].bitcast(FP8X4), scales=ws_scales[:, g, :], in_=ws_grouped[g][:])
+
+        def order_wd_words(g, c):
+            nc.vector.tensor_copy(
+                out=wd_words[g][:, c, :].rearrange("p (t m b) -> p t m b", t=4, b=2),
+                in_=wd_raw[g][:, c, :].rearrange("p (m t b) -> p t m b", t=4, b=2),
+            )
+
+        def order_wd_scales(g):
+            src = sraw_first[:, :, g * W : (g + 1) * W] if g < 2 else sraw_rest[:, :, (g - 2) * W : (g - 1) * W]
+            nc.vector.tensor_copy(
+                out=wd_scales[g][:].rearrange("p c (t m) -> p c t m", t=4),
+                in_=src.rearrange("p c (m t) -> p c t m", t=4),
+            )
+
+        def multiply(g, h, t, c):
+            if c == 0:
+                acc[g, h, t] = acc_pool.tile([P, W], F32, name="acc%d" % t, tag="acc%d" % t)
+            cols = slice(t * P, (t + 1) * P)
+            if c == 0:
+                lhs, lhs_scale = ws_codes[:, g, cols].bitcast(FP8X4), ws_scales[:, g, cols]
+            else:
+                lhs = wd_words[g][:, c - 1, 2 * P * t : 2 * P * (t + 1)].bitcast(FP4X4)
+                lhs_scale = wd_scales[g][:, c - 1, cols]
+            px = slice(h * W, (h + 1) * W)
+            nc.tensor.matmul_mx(
+                out=acc[g, h, t][:], lhsT=lhs, lhsT_scale=lhs_scale,
+                rhs=x_codes[:, c, px].bitcast(FP8X4), rhs_scale=x_scales[:, c, px],
+                start=(c == 0), stop=(c == PASSES - 1),
+            )
+
+        def relu_out(g, h, t):
+            if t == 0:
+                act_out[g, h] = deep3.tile([P, 4, W], F32, name="act_out", tag="act_out")
+            nc.scalar.activation(
+                out=act_out[g, h][:, t, :], in_=acc[g, h, t][:], func=ACT.Relu,
+                bias=affine[:, 8 + g, t : t + 1], scale=affine[:, g, t : t + 1],
+            )
+
+        def clamp(out, in_):
+            nc.vector.tensor_scalar(out=out, in0=in_, scalar1=CAP, scalar2=0.0, op0=ALU.min, op1=ALU.max)
+
+        def clamp_early(g, h, ts, first_tile):
+            part = act_out[g, h][:, ts, first_tile * P : W]
+            clamp(part, part)
+
+        def turn_y(g, h, i, t):
+            if t == 0:
+                banks["y", g, h, i] = turn_pool.tile([P, W], F32, name="bank", tag="bank")
+            nc.tensor.transpose(banks["y", g, h, i][:, t * P : (t + 1) * P], act_out[g, h][:, t, i * P : (i + 1) * P], ident[:])
+
+        def empty_y(g, h, i, on_vector):
+            if (g, h) not in y_out:
+                y_out[g, h] = deep3.tile([P, 4, W], F32, name="y_out", tag="y_out")
+            dst = y_out[g, h][:, i, :].rearrange("r (p t) -> r p t", t=4)
+            src = banks["y", g, h, i][:].rearrange("r (t p) -> r p t", t=4)
+            if on_vector:
+                clamp(dst, src)
+            else:
+                nc.scalar.copy(out=dst, in_=src)
+
+        def group_y(g, h):
+            y_bf[g, h] = stage.tile([P, 4 * W], BF16, name="y_bf", tag="y_bf", align_bytes=64)
+            if POOL:
+                cut = POOL * P
+                dst = y_bf[g, h][:].rearrange("p (m t) -> p m t", t=4)
+                src = act_out[g, h][:].rearrange("p t m -> p m t")
+                nc.gpsimd.tensor_scalar(out=dst[:, 0:cut, :], in0=src[:, 0:cut, :], scalar1=CAP, scalar2=0.0, op0=ALU.min, op1=ALU.max)
+            elif TRICK:
+                clamp(
+                    y_bf[g, h][:].rearrange("p (m i t) -> p m t i", i=4, t=4),
+                    act_out[g, h][:].rearrange("p t (m i) -> p m t i", i=4),
+                )
+            else:
+                clamp(y_bf[g, h][:].rearrange("p (m t) -> p m t", t=4), act_out[g, h][:].rearrange("p t m -> p m t"))
+
+        def quantize_y(g, h):
+            y_codes[g, h] = deep3.tile([P, W], U32, name="y_codes", tag="y_codes", align_bytes=64)
+            if h == 0:
+                y_scales[g] = stage.tile([P, PIXELS], U8, name="y_scales", tag="y_scales", align_bytes=64)
+            nc.vector.quantize_mx(
+                out=y_codes[g, h][:].bitcast(FP8X4), scales=y_scales[g][:, h * W : (h + 1) * W], in_=y_bf[g, h][:]
+            )
+
+        def store_y(g, h, i0, n):
+            dst = y_hbm[h * W : (h + 1) * W, g * W : (g + 1) * W].rearrange("(i p) n -> p i n", p=P)
+            nc.sync.dma_start(out=dst[:, i0 : i0 + n, :], in_=y_out[g, h][:, i0 : i0 + n, :])
+
+        def store_planes(g, h):
+            dst = out_1[g].rearrange("p m t -> p (m t)").bitcast(I32)
+            nc.sync.dma_start(out=dst[:, h * W : (h + 1) * W], in_=y_codes[g, h][:].bitcast(I32))
+            if h == HALVES - 1:
+                for q in range(4):
+                    nc.sync.dma_start(
+                        out=out_2[g, 4 * q : 4 * q + 4, :].bitcast(I32),
+                        in_=y_scales[g][32 * q : 32 * q + 4, :].bitcast(I32),
+                    )
+
+        nc.vector.memset(sraw_first[:].rearrange("p c n -> p (c n)").bitcast(I32), 0)
+        nc.vector.memset(vec_rows[:].bitcast(I32), 0)
+        nc.vector.memset(sraw_rest[:].rearrange("p c n -> p (c n)").bitcast(I32), 0)
+        make_identity(nc, ident[:])
+        nc.gpsimd.dma_start(out=vec_rows[0:GROUPS, :], in_=scale.rearrange("(g n) -> g n", n=W))
+        nc.gpsimd.dma_start(out=vec_rows[8 : 8 + GROUPS, :], in_=shift.rearrange("(g n) -> g n", n=W))
+        load_x(0, 0, 2)
+        load_ws(0, 1)
+        load_x(0, 1, 2)
+        load_wd(0, 1)
+        load_scale_rows(sraw_first, slice(0, 2 * W))
+        load_x(0, 2, 2)
+        load_wd(1, 1)
+        load_x(1, 0, 1)
+        load_ws(1, 1)
+        load_x(1, 1, 1)
+        load_x(1, 2, 1)
+        load_wd(2, 2)
+        load_ws(2, 2)
+        load_scale_rows(sraw_rest, slice(2 * W, C_OUT))
+        load_wd(4, 2)
+        load_ws(4, 2)
+
+        def turn_affine():
+            vec_bank = turn_pool.tile([P, W], F32, name="bank", tag="bank")
+            vec_words = vec_rows[:].bitcast(F32)
+            for u in range(2):
+                nc.tensor.transpose(vec_bank[:, u * P : (u + 1) * P], vec_words[:, u : 2 * P : 2], ident[:])
+            nc.scalar.activation(
+                out=affine[:].rearrange("p r (u e) -> p u r e", u=2),
+                in_=vec_bank[:, 0 : 2 * P].bitcast(BF16).rearrange("p (u r e) -> p u r e", u=2, e=2)[:, :, 0:16, :],
+                func=ACT.Copy,
+            )
+
+        def turn_and_copy_x(h, c, on_vector):
+            for b in range(2):
+                turn_x(h, c, b)
+                copy_x(h, c, b, on_vector[b])
+
+        def passes(c, ts):
+            for t in ts:
+                multiply(0, 0, t, c)
+
+        first_act = 4 - N_ACT
+        turn_and_copy_x(0, 0, (False, False))
+        group_ws(0, 0, 3, True)
+        group_ws(0, 3, 1, False)
+        quantize_x(0, 0)
+        quantize_ws(0)
+        turn_x(0, 1, 0)
+        copy_x(0, 1, 0, False)
+        passes(0, range(4))
+        turn_x(0, 1, 1)
+        copy_x(0, 1, 1, False)
+        order_wd_words(0, 0)
+        order_wd_scales(0)
+        quantize_x(0, 1)
+        turn_and_copy_x(0, 2, (False, False))
+        order_wd_words(0, 1)
+        passes(1, range(4))
+        order_wd_scales(1)
+        order_wd_words(1, 0)
+        quantize_x(0, 2)
+        order_wd_words(1, 1)
+        turn_and_copy_x(1, 0, (False, False))
+        turn_affine()
+        passes(2, range(4))
+        group_ws(1, 0, 4, True)
+        quantize_x(1, 0)
+        turn_and_copy_x(1, 1, (False, True))
+        relu_out(0, 0, 0)
+        quantize_ws(1)
+        quantize_x(1, 1)
+        turn_and_copy_x(1, 2, (False, True))
+        relu_out(0, 0, 1)
+        relu_out(0, 0, 2)
+        quantize_x(1, 2)
+
+        units = [(g, h) for g in range(GROUPS) for h in range(HALVES)]
+
+        def prepare(s, piece):
+            wg = (s + 3) // 2
+            if wg < GROUPS:
+                if s % 2 == 1:
+                    order_wd_words(wg, piece)
+                elif piece == 0:
+                    order_wd_scales(wg)
+                else:
+                    quantize_ws(wg)
+
+        def prepare_act(s, piece):
+            wg = (s + 3) // 2
+            if wg < GROUPS:
+                if s % 2 == 1:
+                    group_ws(wg, piece, 1, False)
+                elif piece == 0:
+                    group_ws(wg, 2, 2, False)
+
+        def clamp_last(ts):
+            part = act_out[units[-1]][:, ts, 0 : 3 * P]
+            clamp(part, part)
+
+        for s in range(1, len(units)):
+            g, h = units[s]
+            pg, ph = units[s - 1]
+            k = K if s < len(units) - 1 else KLAST
+            relu_out(pg, ph, 3)
+            if POOL:
+                group_y(pg, ph)
+            if N_ACT:
+                clamp_early(pg, ph, slice(0, 4), first_act)
+            prepare_act(s, 0)
+            for t in range(k):
+                for c in range(PASSES):
+                    multiply(g, h, t, c)
+                if t < 3:
+                    relu_out(g, h, t)
+            for i in range(4):
+                for t in range(4):
+                    turn_y(pg, ph, i, t)
+            for t in range(k, 4):
+                for c in range(PASSES):
+                    multiply(g, h, t, c)
+            prepare(s, 0)
+            if not POOL:
+                group_y(pg, ph)
+            if s == len(units) - 1:
+                clamp_last(slice(0, 2))
+            for i in range(4):
+                empty_y(pg, ph, i, i < first_act)
+            store_y(pg, ph, 0, 4)
+            quantize_y(pg, ph)
+            store_planes(pg, ph)
+            for t in range(k, 3):
+                relu_out(g, h, t)
+            prepare_act(s, 1)
+            prepare(s, 1)
+
+        g, h = units[-1]
+        clamp_last(slice(2, 3))
+        relu_out(g, h, 3)
+        clamp_last(slice(3, 4))
+        for t in range(4):
+            for i in range(4):
+                turn_y(g, h, i, t)
+        y_bf[g, h] = stage.tile([P, 4 * W], BF16, name="y_bf", tag="y_bf", align_bytes=64)
+        clamp(
+            y_bf[g, h][:].rearrange("p (m i t) -> p m t i", i=4, t=4),
+            act_out[g, h][:].rearrange("p t (m i) -> p m t i", i=4),
+        )
+        for i in range(3):
+            empty_y(g, h, i, False)
+        empty_y(g, h, 3, True)
+        quantize_y(g, h)
+        for i in (0, 3, 1):
+            store_y(g, h, i, 1)
+        store_planes(g, h)
+        store_y(g, h, 2, 1)

@@ -26,6 +26,9 @@ TRICK = True
 K = 3
 KLAST = 2
 POOL = 0
+NV = 1
+KLATE = 3
+TAILV = 0
 
 
 def tile_skip_expand_relu6_g5_kernel(
@@ -48,35 +51,27 @@ def tile_skip_expand_relu6_g5_kernel(
         vec_rows = keep.tile([P, W], BF16, name="vec_rows")
         affine = keep.tile([P, 16, 4], F32, name="affine")
         x_raw = {}
-        for h in range(HALVES):
-            for c in range(PASSES):
-                x_raw[h, c] = keep.tile([P, 4, W], BF16, name="x_raw_%d_%d" % (h, c))
         x_codes = keep.tile([P, PASSES, PIXELS], U32, name="x_codes", align_bytes=64)
         x_scales = keep.tile([P, PASSES, PIXELS], U8, name="x_scales", align_bytes=64)
-        ws_raw, wd_raw, wd_words, wd_scales = {}, {}, {}, {}
+        ws_raw, wd_raw, wd_first, wd_words, wd_scales = {}, {}, {}, {}, {}
         for g in range(GROUPS):
             wd_words[g] = keep.tile([P, 2, 2 * W], U8, name="wd_words_%d" % g, align_bytes=64)
             wd_scales[g] = keep.tile([P, 2, W], U8, name="wd_scales_%d" % g, align_bytes=64)
         ws_codes = keep.tile([P, GROUPS, W], U32, name="ws_codes", align_bytes=64)
         ws_scales = keep.tile([P, GROUPS, W], U8, name="ws_scales", align_bytes=64)
-        sraw_first = keep.tile([P, 2, 2 * W], U8, name="sraw_first")
-        sraw_rest = keep.tile([P, 2, C_OUT - 2 * W], U8, name="sraw_rest")
+        sraw_first = keep.tile([P, 2, W], U8, name="sraw_first")
+        sraw_rest = keep.tile([P, 2, W], U8, name="sraw_rest")
+        sord_rest = keep.tile([P, 2, W], U8, name="sord_rest")
 
         x_grouped, ws_grouped, acc, act_out, banks, y_out, y_bf, y_codes, y_scales = {}, {}, {}, {}, {}, {}, {}, {}, {}
 
-        def load_x(h, c, pieces):
-            rows = slice(h * W, (h + 1) * W)
-            src = x_skip[rows, :] if c == 0 else x_deep[rows, (c - 1) * W : c * W]
-            src = src.rearrange("(b p i) k -> p b i k", p=P, i=2)
-            dst = x_raw[h, c][:].rearrange("p (b i) k -> p b i k", i=2)
-            if pieces == 2:
-                for b in range(2):
-                    nc.sync.dma_start(out=dst[:, b, :, :], in_=src[:, b, :, :])
-            elif c == 0:
-                nc.sync.dma_start(out=dst.rearrange("p b i k -> p b (i k)"), in_=src.rearrange("p b i k -> p b (i k)"))
-            else:
-                for b in range(2):
-                    nc.sync.dma_start(out=dst[:, b, :, :], in_=src[:, b, :, :])
+        def load_x(src, h, b, first_pass):
+            width = src.shape[1]
+            raw = keep.tile([P, 2, width], BF16, name="x_raw_%d_%d_%d" % (first_pass, h, b))
+            rows = slice(h * W + b * 2 * P, h * W + (b + 1) * 2 * P)
+            nc.sync.dma_start(out=raw[:], in_=src[rows, :].rearrange("(p i) k -> p i k", i=2))
+            for j in range(width // W):
+                x_raw[h, first_pass + j, b] = raw[:, :, j * W : (j + 1) * W]
 
         def load_ws(g, n):
             cols = slice(g * W, (g + n) * W)
@@ -93,28 +88,45 @@ def tile_skip_expand_relu6_g5_kernel(
             for j in range(n):
                 wd_raw[g + j] = raw[:, :, 2 * j * W : 2 * (j + 1) * W]
 
-        def load_scale_rows(tile, cols):
+        def load_wd_first(c):
+            raw = keep.tile([P, 2 * W], U8, name="wd_raw_first_%d" % c)
+            nc.sync.dma_start(out=raw[:].bitcast(I32), in_=w_deep_words[c, :, 0 : 2 * W].bitcast(I32))
+            wd_first[c] = raw
+
+        def load_scale_rows_first():
             for q in range(4):
-                src = w_deep_scales[:, 4 * q : 4 * q + 4, cols].rearrange("c r n -> r c n")
-                nc.sync.dma_start(out=tile[32 * q : 32 * q + 4, :, :].bitcast(I32), in_=src.bitcast(I32))
+                src = w_deep_scales[:, 4 * q : 4 * q + 4, 0:W].rearrange("c r n -> r c n")
+                nc.sync.dma_start(out=sraw_first[32 * q : 32 * q + 4, :, :].bitcast(I32), in_=src.bitcast(I32))
+
+        def load_scale_rows_rest():
+            for g in range(1, GROUPS):
+                src = w_deep_scales[:, :, g * W : (g + 1) * W].rearrange("c q n -> q c n")
+                nc.sync.dma_start(out=sraw_rest[16 * g : 16 * g + 16, :, :].bitcast(I32), in_=src.bitcast(I32))
+
+        def place_scale_rows(g):
+            for q in range(4):
+                nc.sync.dma_start(
+                    out=wd_scales[g][32 * q : 32 * q + 4, :, :].rearrange("r c n -> r (c n)").bitcast(I32),
+                    in_=sord_rest[16 * g + 4 * q : 16 * g + 4 * q + 4, :, :].rearrange("r c n -> r (c n)").bitcast(I32),
+                )
 
         def turn_x(h, c, b):
             bank = turn_pool.tile([P, W], F32, name="bank", tag="bank")
             banks["x", h, c, b] = bank
             for i in range(2):
-                words = x_raw[h, c][:, 2 * b + i, :].bitcast(F32)
+                words = x_raw[h, c, b][:, i, :].bitcast(F32)
                 for u in range(2):
                     j = 2 * i + u
                     nc.tensor.transpose(bank[:, j * P : (j + 1) * P], words[:, u : 2 * P : 2], ident[:])
 
         def copy_x(h, c, b, on_vector):
-            if b == 0:
-                x_grouped[h, c] = stage.tile([P, 4 * W], BF16, name="x_grouped", tag="x_grouped", align_bytes=64)
+            if (h, c) not in x_grouped:
+                x_grouped[h, c] = deep3.tile([P, 4 * W], BF16, name="x_grouped", tag="x_grouped", align_bytes=64)
             dst = x_grouped[h, c][:, b * 2 * W : (b + 1) * 2 * W].bitcast(F32).rearrange("p (r j) -> p r j", j=4)
             src = banks["x", h, c, b][:].rearrange("p (j r) -> p r j", j=4)
             if on_vector:
                 nc.vector.tensor_copy(out=dst, in_=src)
-            elif (h, c, b) == (0, 0, 0):
+            elif (h, c, b) == (0, 1, 0):
                 nc.scalar.activation(
                     out=x_grouped[h, c][:, 0 : 2 * W].rearrange("p (r j e) -> p r j e", j=4, e=2),
                     in_=banks["x", h, c, b][:].bitcast(BF16).rearrange("p (j r e) -> p r j e", j=4, e=2),
@@ -131,7 +143,7 @@ def tile_skip_expand_relu6_g5_kernel(
             )
 
         def group_ws(g, t, n, on_vector):
-            if t == 0:
+            if g not in ws_grouped:
                 ws_grouped[g] = stage.tile([P, 4 * W], BF16, name="ws_grouped", tag="ws_grouped", align_bytes=64)
             dst = ws_grouped[g][:].rearrange("p (t m j) -> p t m j", t=4, j=4)[:, t : t + n, :, :]
             src = ws_raw[g].rearrange("p j (m t) -> p t m j", t=4)[:, t : t + n, :, :]
@@ -146,18 +158,19 @@ def tile_skip_expand_relu6_g5_kernel(
         def order_wd_words(g, c):
             nc.vector.tensor_copy(
                 out=wd_words[g][:, c, :].rearrange("p (t m b) -> p t m b", t=4, b=2),
-                in_=wd_raw[g][:, c, :].rearrange("p (m t b) -> p t m b", t=4, b=2),
+                in_=(wd_raw[g][:, c, :] if g else wd_first[c][:]).rearrange("p (m t b) -> p t m b", t=4, b=2),
             )
 
         def order_wd_scales(g):
-            src = sraw_first[:, :, g * W : (g + 1) * W] if g < 2 else sraw_rest[:, :, (g - 2) * W : (g - 1) * W]
+            src = sraw_first[:] if g == 0 else sraw_rest[:]
             nc.vector.tensor_copy(
-                out=wd_scales[g][:].rearrange("p c (t m) -> p c t m", t=4),
+                out=(wd_scales[0] if g == 0 else sord_rest)[:].rearrange("p c (t m) -> p c t m", t=4),
                 in_=src.rearrange("p c (m t) -> p c t m", t=4),
             )
 
-        def multiply(g, h, t, c):
-            if c == 0:
+        def multiply(g, h, t, j):
+            c = (j + 1) % PASSES if (g, h) == (0, 0) else j
+            if j == 0:
                 acc[g, h, t] = acc_pool.tile([P, W], F32, name="acc%d" % t, tag="acc%d" % t)
             cols = slice(t * P, (t + 1) * P)
             if c == 0:
@@ -169,14 +182,14 @@ def tile_skip_expand_relu6_g5_kernel(
             nc.tensor.matmul_mx(
                 out=acc[g, h, t][:], lhsT=lhs, lhsT_scale=lhs_scale,
                 rhs=x_codes[:, c, px].bitcast(FP8X4), rhs_scale=x_scales[:, c, px],
-                start=(c == 0), stop=(c == PASSES - 1),
+                start=(j == 0), stop=(j == PASSES - 1),
             )
 
-        def relu_out(g, h, t):
-            if t == 0:
+        def relu_out(g, h, t, px=slice(0, W)):
+            if (g, h) not in act_out:
                 act_out[g, h] = deep3.tile([P, 4, W], F32, name="act_out", tag="act_out")
             nc.scalar.activation(
-                out=act_out[g, h][:, t, :], in_=acc[g, h, t][:], func=ACT.Relu,
+                out=act_out[g, h][:, t, px], in_=acc[g, h, t][:, px], func=ACT.Relu,
                 bias=affine[:, 8 + g, t : t + 1], scale=affine[:, g, t : t + 1],
             )
 
@@ -188,7 +201,7 @@ def tile_skip_expand_relu6_g5_kernel(
             clamp(part, part)
 
         def turn_y(g, h, i, t):
-            if t == 0:
+            if ("y", g, h, i) not in banks:
                 banks["y", g, h, i] = turn_pool.tile([P, W], F32, name="bank", tag="bank")
             nc.tensor.transpose(banks["y", g, h, i][:, t * P : (t + 1) * P], act_out[g, h][:, t, i * P : (i + 1) * P], ident[:])
 
@@ -231,169 +244,203 @@ def tile_skip_expand_relu6_g5_kernel(
 
         def store_planes(g, h):
             dst = out_1[g].rearrange("p m t -> p (m t)").bitcast(I32)
-            nc.sync.dma_start(out=dst[:, h * W : (h + 1) * W], in_=y_codes[g, h][:].bitcast(I32))
             if h == HALVES - 1:
                 for q in range(4):
                     nc.sync.dma_start(
                         out=out_2[g, 4 * q : 4 * q + 4, :].bitcast(I32),
                         in_=y_scales[g][32 * q : 32 * q + 4, :].bitcast(I32),
                     )
+            nc.sync.dma_start(out=dst[:, h * W : (h + 1) * W], in_=y_codes[g, h][:].bitcast(I32))
 
+        units = [(g, h) for g in range(GROUPS) for h in range(HALVES)]
+        first_act = 4 - N_ACT
         nc.vector.memset(sraw_first[:].rearrange("p c n -> p (c n)").bitcast(I32), 0)
         nc.vector.memset(vec_rows[:].bitcast(I32), 0)
         nc.vector.memset(sraw_rest[:].rearrange("p c n -> p (c n)").bitcast(I32), 0)
+        for g in range(1, GROUPS):
+            nc.vector.memset(wd_scales[g][:].rearrange("p c n -> p (c n)").bitcast(I32), 0)
         make_identity(nc, ident[:])
         nc.gpsimd.dma_start(out=vec_rows[0:GROUPS, :], in_=scale.rearrange("(g n) -> g n", n=W))
         nc.gpsimd.dma_start(out=vec_rows[8 : 8 + GROUPS, :], in_=shift.rearrange("(g n) -> g n", n=W))
-        load_x(0, 0, 2)
-        load_ws(0, 1)
-        load_x(0, 1, 2)
-        load_wd(0, 1)
-        load_scale_rows(sraw_first, slice(0, 2 * W))
-        load_x(0, 2, 2)
-        load_wd(1, 1)
-        load_x(1, 0, 1)
-        load_ws(1, 1)
-        load_x(1, 1, 1)
-        load_x(1, 2, 1)
-        load_wd(2, 2)
-        load_ws(2, 2)
-        load_scale_rows(sraw_rest, slice(2 * W, C_OUT))
-        load_wd(4, 2)
-        load_ws(4, 2)
 
         def turn_affine():
-            vec_bank = turn_pool.tile([P, W], F32, name="bank", tag="bank")
+            banks["affine"] = turn_pool.tile([P, W], F32, name="bank", tag="bank")
             vec_words = vec_rows[:].bitcast(F32)
             for u in range(2):
-                nc.tensor.transpose(vec_bank[:, u * P : (u + 1) * P], vec_words[:, u : 2 * P : 2], ident[:])
+                nc.tensor.transpose(banks["affine"][:, u * P : (u + 1) * P], vec_words[:, u : 2 * P : 2], ident[:])
+
+        def copy_affine():
             nc.scalar.activation(
                 out=affine[:].rearrange("p r (u e) -> p u r e", u=2),
-                in_=vec_bank[:, 0 : 2 * P].bitcast(BF16).rearrange("p (u r e) -> p u r e", u=2, e=2)[:, :, 0:16, :],
+                in_=banks["affine"][:, 0 : 2 * P].bitcast(BF16).rearrange("p (u r e) -> p u r e", u=2, e=2)[:, :, 0:16, :],
                 func=ACT.Copy,
             )
 
-        def turn_and_copy_x(h, c, on_vector):
-            for b in range(2):
-                turn_x(h, c, b)
-                copy_x(h, c, b, on_vector[b])
+        def clamp_last(t):
+            part = act_out[units[-1]][:, t, NV * P : W]
+            clamp(part, part)
 
-        def passes(c, ts):
+        def turn_tile(g, h, i):
+            for t in range(4):
+                turn_y(g, h, i, t)
+
+        def turn_last(t):
+            for i in range(4):
+                turn_y(GROUPS - 1, HALVES - 1, i, t)
+
+        load_x(x_deep[:, 0:W], 0, 0, 1)
+        load_wd_first(0)
+        load_scale_rows_first()
+        load_x(x_deep[:, 0:W], 0, 1, 1)
+        load_x(x_deep[:, W : 2 * W], 0, 0, 2)
+        load_x(x_deep[:, W : 2 * W], 0, 1, 2)
+        load_wd_first(1)
+        load_x(x_skip, 0, 0, 0)
+        load_x(x_skip, 0, 1, 0)
+        load_wd(1, 1)
+        load_ws(0, 1)
+        load_x(x_skip, 1, 0, 0)
+        load_x(x_skip, 1, 1, 0)
+        load_scale_rows_rest()
+        load_x(x_deep, 1, 0, 1)
+        load_x(x_deep, 1, 1, 1)
+        load_ws(1, 1)
+
+        def tx(h, c, b, on_vector=False):
+            turn_x(h, c, b)
+            copy_x(h, c, b, on_vector)
+
+        def passes(j, ts):
             for t in ts:
-                multiply(0, 0, t, c)
+                multiply(0, 0, t, j)
 
-        first_act = 4 - N_ACT
-        turn_and_copy_x(0, 0, (False, False))
-        group_ws(0, 0, 3, True)
-        group_ws(0, 3, 1, False)
-        quantize_x(0, 0)
-        quantize_ws(0)
-        turn_x(0, 1, 0)
-        copy_x(0, 1, 0, False)
-        passes(0, range(4))
-        turn_x(0, 1, 1)
-        copy_x(0, 1, 1, False)
+        tx(0, 1, 0)
         order_wd_words(0, 0)
         order_wd_scales(0)
-        quantize_x(0, 1)
-        turn_and_copy_x(0, 2, (False, False))
+        tx(0, 1, 1)
+        quantize_x(0, 1, 0, 1)
+        quantize_x(0, 1, 1, 1)
+        tx(0, 2, 0)
+        passes(0, (0, 1))
+        tx(0, 2, 1)
         order_wd_words(0, 1)
-        passes(1, range(4))
-        order_wd_scales(1)
         order_wd_words(1, 0)
-        quantize_x(0, 2)
         order_wd_words(1, 1)
-        turn_and_copy_x(1, 0, (False, False))
-        turn_affine()
-        passes(2, range(4))
-        group_ws(1, 0, 4, True)
+        passes(0, (2, 3))
+        quantize_x(0, 2)
+        tx(0, 0, 0)
+        tx(0, 0, 1)
+        group_ws(0, 0, 3, True)
+        group_ws(0, 3, 1, False)
+        passes(1, (0, 1))
+        quantize_x(0, 0)
+        tx(1, 0, 0)
+        tx(1, 0, 1)
+        quantize_ws(0)
+        order_wd_scales(1)
+        load_ws(2, 1)
+        load_wd(2, 2)
+        place_scale_rows(1)
+        passes(1, (2, 3))
         quantize_x(1, 0)
-        turn_and_copy_x(1, 1, (False, True))
+        turn_affine()
+        copy_affine()
+        tx(1, 1, 0, True)
+        tx(1, 1, 1)
+        passes(2, (0, 1))
         relu_out(0, 0, 0)
-        quantize_ws(1)
-        quantize_x(1, 1)
-        turn_and_copy_x(1, 2, (False, True))
         relu_out(0, 0, 1)
+        quantize_x(1, 1)
+        tx(1, 2, 0, True)
+        tx(1, 2, 1)
+        passes(2, (2, 3))
         relu_out(0, 0, 2)
+        group_ws(1, 0, 2, True)
         quantize_x(1, 2)
-
-        units = [(g, h) for g in range(GROUPS) for h in range(HALVES)]
+        group_ws(1, 2, 2, True)
+        load_ws(3, 1)
+        place_scale_rows(2)
+        load_wd(4, 2)
+        place_scale_rows(3)
+        load_ws(4, 2)
+        place_scale_rows(4)
+        place_scale_rows(5)
 
         def prepare(s, piece):
             wg = (s + 3) // 2
-            if wg < GROUPS:
-                if s % 2 == 1:
-                    order_wd_words(wg, piece)
-                elif piece == 0:
-                    order_wd_scales(wg)
-                else:
-                    quantize_ws(wg)
+            if s % 2 == 1 and wg < GROUPS:
+                order_wd_words(wg, piece)
+            elif s % 2 == 0 and piece == 1 and wg < GROUPS:
+                quantize_ws(wg)
 
         def prepare_act(s, piece):
             wg = (s + 3) // 2
             if wg < GROUPS:
-                if s % 2 == 1:
-                    group_ws(wg, piece, 1, False)
-                elif piece == 0:
-                    group_ws(wg, 2, 2, False)
+                group_ws(wg, 2 * ((s + 1) % 2) + piece, 1, False)
 
-        def clamp_last(ts):
-            part = act_out[units[-1]][:, ts, 0 : 3 * P]
-            clamp(part, part)
-
+        tile_order = list(range(first_act, 4)) + list(range(first_act))
         for s in range(1, len(units)):
             g, h = units[s]
             pg, ph = units[s - 1]
-            k = K if s < len(units) - 1 else KLAST
+            last = s == len(units) - 1
+            k = KLAST if last else (KLATE if s >= 9 else K)
             relu_out(pg, ph, 3)
-            if POOL:
-                group_y(pg, ph)
-            if N_ACT:
-                clamp_early(pg, ph, slice(0, 4), first_act)
+            clamp_early(pg, ph, slice(0, 4), first_act)
+            if s == 1:
+                quantize_ws(1)
             prepare_act(s, 0)
+            if s == 1:
+                for j in range(PASSES):
+                    for t in range(k):
+                        multiply(g, h, t, j)
             for t in range(k):
-                for c in range(PASSES):
-                    multiply(g, h, t, c)
-                if t < 3:
-                    relu_out(g, h, t)
-            for i in range(4):
-                for t in range(4):
-                    turn_y(pg, ph, i, t)
+                for j in range(PASSES if s > 1 else 0):
+                    multiply(g, h, t, j)
+                relu_out(g, h, t)
+            for i in tile_order:
+                turn_tile(pg, ph, i)
             for t in range(k, 4):
-                for c in range(PASSES):
-                    multiply(g, h, t, c)
+                for j in range(PASSES):
+                    multiply(g, h, t, j)
             prepare(s, 0)
-            if not POOL:
-                group_y(pg, ph)
-            if s == len(units) - 1:
-                clamp_last(slice(0, 2))
-            for i in range(4):
+            group_y(pg, ph)
+            for i in tile_order:
                 empty_y(pg, ph, i, i < first_act)
-            store_y(pg, ph, 0, 4)
+            store_y(pg, ph, 2, 2)
+            store_y(pg, ph, 0, 2)
+            if last:
+                for t in range(k):
+                    clamp_last(t)
             quantize_y(pg, ph)
             store_planes(pg, ph)
             for t in range(k, 3):
                 relu_out(g, h, t)
+                if last:
+                    clamp_last(t)
             prepare_act(s, 1)
             prepare(s, 1)
 
         g, h = units[-1]
-        clamp_last(slice(2, 3))
-        relu_out(g, h, 3)
-        clamp_last(slice(3, 4))
-        for t in range(4):
-            for i in range(4):
+        relu_out(g, h, 3, slice(0, NV * P))
+        relu_out(g, h, 3, slice(NV * P, W))
+        for i in range(2):
+            for t in range(3):
                 turn_y(g, h, i, t)
-        y_bf[g, h] = stage.tile([P, 4 * W], BF16, name="y_bf", tag="y_bf", align_bytes=64)
-        clamp(
-            y_bf[g, h][:].rearrange("p (m i t) -> p m t i", i=4, t=4),
-            act_out[g, h][:].rearrange("p t (m i) -> p m t i", i=4),
-        )
-        for i in range(3):
-            empty_y(g, h, i, False)
-        empty_y(g, h, 3, True)
+        turn_y(g, h, 0, 3)
+        for i in range(2, 4):
+            for t in range(3):
+                turn_y(g, h, i, t)
+        if TAILV == 0:
+            clamp_last(3)
+        empty_y(g, h, 0, True)
+        if TAILV == 1:
+            clamp_last(3)
+        for i in range(1, 4):
+            turn_y(g, h, i, 3)
+        for i in range(1, 4):
+            empty_y(g, h, i, i < NV)
+        group_y(g, h)
         quantize_y(g, h)
-        for i in (0, 3, 1):
+        for i in ((0, 1, 2, 3) if NV == 1 else (0, 2, 1, 3)):
             store_y(g, h, i, 1)
         store_planes(g, h)
-        store_y(g, h, 2, 1)

@@ -15,20 +15,20 @@ ACT = mybir.ActivationFunctionType
 
 PIXELS, C_SKIP, C_DEEP, C_OUT = 1024, 512, 1024, 3072
 FLOPS = 2 * PIXELS * (C_SKIP + C_DEEP) * C_OUT
+CAP = 6.0
+
 P = 128
 W = 512
+SLOTS = 4
+TILES = W // P
 GROUPS = C_OUT // W
 HALVES = PIXELS // W
+SKIP, DEEP_LO, DEEP_HI = 0, 1, 2
 PASSES = 3
-CAP = 6.0
-N_ACT = 2
-TRICK = True
-K = 3
-KLAST = 2
-POOL = 0
-NV = 1
-KLATE = 3
-TAILV = 0
+SHIFT_ROW = 8
+AFFINE_ROWS = 16
+VECTOR_TILES, SCALAR_TILES = (0, 1), (2, 3)
+SLOTS_BEFORE_TURN, SLOTS_BEFORE_TURN_LAST = 2, 1
 
 
 def tile_skip_expand_relu6_g5_kernel(
@@ -41,29 +41,30 @@ def tile_skip_expand_relu6_g5_kernel(
 
     with ExitStack() as ctx:
         keep = ctx.enter_context(tc.tile_pool(name="keep", bufs=1))
-        stage = ctx.enter_context(tc.tile_pool(name="stage", bufs=2))
-        deep3 = ctx.enter_context(tc.tile_pool(name="deep3", bufs=3))
+        double = ctx.enter_context(tc.tile_pool(name="double", bufs=2))
+        triple = ctx.enter_context(tc.tile_pool(name="triple", bufs=3))
         acc_pool = ctx.enter_context(tc.psum_pool(name="acc", bufs=1))
         turn_pool = ctx.enter_context(tc.psum_pool(name="turn", bufs=4))
         ctx.enter_context(tc.manual_schedule())
 
         ident = keep.tile([P, P], F32, name="ident")
-        vec_rows = keep.tile([P, W], BF16, name="vec_rows")
-        affine = keep.tile([P, 16, 4], F32, name="affine")
-        x_raw = {}
+        affine_rows = keep.tile([P, W], BF16, name="affine_rows")
+        affine = keep.tile([P, AFFINE_ROWS, SLOTS], F32, name="affine")
         x_codes = keep.tile([P, PASSES, PIXELS], U32, name="x_codes", align_bytes=64)
         x_scales = keep.tile([P, PASSES, PIXELS], U8, name="x_scales", align_bytes=64)
-        ws_raw, wd_raw, wd_first, wd_words, wd_scales = {}, {}, {}, {}, {}
+        wd_words, wd_scales = {}, {}
         for g in range(GROUPS):
             wd_words[g] = keep.tile([P, 2, 2 * W], U8, name="wd_words_%d" % g, align_bytes=64)
             wd_scales[g] = keep.tile([P, 2, W], U8, name="wd_scales_%d" % g, align_bytes=64)
         ws_codes = keep.tile([P, GROUPS, W], U32, name="ws_codes", align_bytes=64)
         ws_scales = keep.tile([P, GROUPS, W], U8, name="ws_scales", align_bytes=64)
-        sraw_first = keep.tile([P, 2, W], U8, name="sraw_first")
-        sraw_rest = keep.tile([P, 2, W], U8, name="sraw_rest")
-        sord_rest = keep.tile([P, 2, W], U8, name="sord_rest")
+        scale_rows_first = keep.tile([P, 2, W], U8, name="scale_rows_first")
+        scale_rows_later = keep.tile([P, 2, W], U8, name="scale_rows_later")
+        scale_rows_ordered = keep.tile([P, 2, W], U8, name="scale_rows_ordered")
 
-        x_grouped, ws_grouped, acc, act_out, banks, y_out, y_bf, y_codes, y_scales = {}, {}, {}, {}, {}, {}, {}, {}, {}
+        x_raw, ws_raw, wd_raw = {}, {}, {}
+        x_grouped, ws_grouped, acc, relu, banks, y_out, y_bf, y_codes, y_scales = {}, {}, {}, {}, {}, {}, {}, {}, {}
+
 
         def load_x(src, h, b, first_pass):
             width = src.shape[1]
@@ -75,78 +76,83 @@ def tile_skip_expand_relu6_g5_kernel(
 
         def load_ws(g, n):
             cols = slice(g * W, (g + n) * W)
-            raw = keep.tile([P, 4, n * W], BF16, name="ws_raw_%d" % g)
-            nc.sync.dma_start(out=raw[:], in_=w_skip[:, cols].rearrange("(p j) n -> p j n", j=4))
+            raw = keep.tile([P, SLOTS, n * W], BF16, name="ws_raw_%d" % g)
+            nc.sync.dma_start(out=raw[:], in_=w_skip[:, cols].rearrange("(p j) n -> p j n", j=SLOTS))
             for j in range(n):
                 ws_raw[g + j] = raw[:, :, j * W : (j + 1) * W]
 
         def load_wd(g, n):
             cols = slice(2 * g * W, 2 * (g + n) * W)
-            src = w_deep_words[:, :, cols].rearrange("c p b -> p c b")
+            src = w_deep_words[:, :, cols].rearrange("d p b -> p d b")
             raw = keep.tile([P, 2, 2 * n * W], U8, name="wd_raw_%d" % g)
             nc.sync.dma_start(out=raw[:].bitcast(I32), in_=src.bitcast(I32))
             for j in range(n):
-                wd_raw[g + j] = raw[:, :, 2 * j * W : 2 * (j + 1) * W]
+                for d in range(2):
+                    wd_raw[g + j, d] = raw[:, d, 2 * j * W : 2 * (j + 1) * W]
 
-        def load_wd_first(c):
-            raw = keep.tile([P, 2 * W], U8, name="wd_raw_first_%d" % c)
-            nc.sync.dma_start(out=raw[:].bitcast(I32), in_=w_deep_words[c, :, 0 : 2 * W].bitcast(I32))
-            wd_first[c] = raw
+        def load_wd_first(d):
+            raw = keep.tile([P, 2 * W], U8, name="wd_raw_first_%d" % d)
+            nc.sync.dma_start(out=raw[:].bitcast(I32), in_=w_deep_words[d, :, 0 : 2 * W].bitcast(I32))
+            wd_raw[0, d] = raw[:]
 
         def load_scale_rows_first():
-            for q in range(4):
-                src = w_deep_scales[:, 4 * q : 4 * q + 4, 0:W].rearrange("c r n -> r c n")
-                nc.sync.dma_start(out=sraw_first[32 * q : 32 * q + 4, :, :].bitcast(I32), in_=src.bitcast(I32))
+            for quad in range(4):
+                src = w_deep_scales[:, 4 * quad : 4 * quad + 4, 0:W].rearrange("d r n -> r d n")
+                dst = scale_rows_first[32 * quad : 32 * quad + 4, :, :]
+                nc.sync.dma_start(out=dst.bitcast(I32), in_=src.bitcast(I32))
 
-        def load_scale_rows_rest():
+        def load_scale_rows_later():
             for g in range(1, GROUPS):
-                src = w_deep_scales[:, :, g * W : (g + 1) * W].rearrange("c q n -> q c n")
-                nc.sync.dma_start(out=sraw_rest[16 * g : 16 * g + 16, :, :].bitcast(I32), in_=src.bitcast(I32))
+                src = w_deep_scales[:, :, g * W : (g + 1) * W].rearrange("d q n -> q d n")
+                dst = scale_rows_later[16 * g : 16 * g + 16, :, :]
+                nc.sync.dma_start(out=dst.bitcast(I32), in_=src.bitcast(I32))
 
         def place_scale_rows(g):
-            for q in range(4):
-                nc.sync.dma_start(
-                    out=wd_scales[g][32 * q : 32 * q + 4, :, :].rearrange("r c n -> r (c n)").bitcast(I32),
-                    in_=sord_rest[16 * g + 4 * q : 16 * g + 4 * q + 4, :, :].rearrange("r c n -> r (c n)").bitcast(I32),
-                )
+            for quad in range(4):
+                first = 16 * g + 4 * quad
+                src = scale_rows_ordered[first : first + 4, :, :].rearrange("r d n -> r (d n)")
+                dst = wd_scales[g][32 * quad : 32 * quad + 4, :, :].rearrange("r d n -> r (d n)")
+                nc.sync.dma_start(out=dst.bitcast(I32), in_=src.bitcast(I32))
 
-        def turn_x(h, c, b):
+
+        def turn_words(bank, first, words):
+            for u in range(2):
+                nc.tensor.transpose(bank[:, (first + u) * P : (first + u + 1) * P], words[:, u : 2 * P : 2], ident[:])
+
+        def turn_x(h, c, b, on_vector=False, by_activation=False):
             bank = turn_pool.tile([P, W], F32, name="bank", tag="bank")
-            banks["x", h, c, b] = bank
             for i in range(2):
-                words = x_raw[h, c, b][:, i, :].bitcast(F32)
-                for u in range(2):
-                    j = 2 * i + u
-                    nc.tensor.transpose(bank[:, j * P : (j + 1) * P], words[:, u : 2 * P : 2], ident[:])
-
-        def copy_x(h, c, b, on_vector):
-            if (h, c) not in x_grouped:
-                x_grouped[h, c] = deep3.tile([P, 4 * W], BF16, name="x_grouped", tag="x_grouped", align_bytes=64)
-            dst = x_grouped[h, c][:, b * 2 * W : (b + 1) * 2 * W].bitcast(F32).rearrange("p (r j) -> p r j", j=4)
-            src = banks["x", h, c, b][:].rearrange("p (j r) -> p r j", j=4)
-            if on_vector:
-                nc.vector.tensor_copy(out=dst, in_=src)
-            elif (h, c, b) == (0, 1, 0):
+                turn_words(bank, 2 * i, x_raw[h, c, b][:, i, :].bitcast(F32))
+            if b == 0:
+                x_grouped[h, c] = triple.tile([P, SLOTS * W], BF16, name="x_grouped", tag="x_grouped", align_bytes=64)
+            part = x_grouped[h, c][:, b * 2 * W : (b + 1) * 2 * W]
+            if by_activation:
                 nc.scalar.activation(
-                    out=x_grouped[h, c][:, 0 : 2 * W].rearrange("p (r j e) -> p r j e", j=4, e=2),
-                    in_=banks["x", h, c, b][:].bitcast(BF16).rearrange("p (j r e) -> p r j e", j=4, e=2),
+                    out=part.rearrange("p (r j e) -> p r j e", j=4, e=2),
+                    in_=bank[:].bitcast(BF16).rearrange("p (j r e) -> p r j e", j=4, e=2),
                     func=ACT.Copy,
                 )
+                return
+            dst = part.bitcast(F32).rearrange("p (r j) -> p r j", j=4)
+            src = bank[:].rearrange("p (j r) -> p r j", j=4)
+            if on_vector:
+                nc.vector.tensor_copy(out=dst, in_=src)
             else:
                 nc.scalar.copy(out=dst, in_=src)
 
         def quantize_x(h, c, b0=0, n=2):
             cols = slice(h * W + b0 * 2 * P, h * W + (b0 + n) * 2 * P)
             nc.vector.quantize_mx(
-                out=x_codes[:, c, cols].bitcast(FP8X4), scales=x_scales[:, c, cols],
+                out=x_codes[:, c, cols].bitcast(FP8X4),
+                scales=x_scales[:, c, cols],
                 in_=x_grouped[h, c][:, b0 * 2 * W : (b0 + n) * 2 * W],
             )
 
-        def group_ws(g, t, n, on_vector):
-            if g not in ws_grouped:
-                ws_grouped[g] = stage.tile([P, 4 * W], BF16, name="ws_grouped", tag="ws_grouped", align_bytes=64)
-            dst = ws_grouped[g][:].rearrange("p (t m j) -> p t m j", t=4, j=4)[:, t : t + n, :, :]
-            src = ws_raw[g].rearrange("p j (m t) -> p t m j", t=4)[:, t : t + n, :, :]
+        def group_ws(g, t, n, on_vector=False):
+            if t == 0:
+                ws_grouped[g] = double.tile([P, SLOTS * W], BF16, name="ws_grouped", tag="ws_grouped", align_bytes=64)
+            dst = ws_grouped[g][:].rearrange("p (t m j) -> p t m j", t=SLOTS, j=SLOTS)[:, t : t + n, :, :]
+            src = ws_raw[g].rearrange("p j (m t) -> p t m j", t=SLOTS)[:, t : t + n, :, :]
             if on_vector:
                 nc.vector.tensor_copy(out=dst, in_=src)
             else:
@@ -155,209 +161,179 @@ def tile_skip_expand_relu6_g5_kernel(
         def quantize_ws(g):
             nc.vector.quantize_mx(out=ws_codes[:, g, :].bitcast(FP8X4), scales=ws_scales[:, g, :], in_=ws_grouped[g][:])
 
-        def order_wd_words(g, c):
+        def order_wd_words(g, d):
             nc.vector.tensor_copy(
-                out=wd_words[g][:, c, :].rearrange("p (t m b) -> p t m b", t=4, b=2),
-                in_=(wd_raw[g][:, c, :] if g else wd_first[c][:]).rearrange("p (m t b) -> p t m b", t=4, b=2),
+                out=wd_words[g][:, d, :].rearrange("p (t m b) -> p t m b", t=SLOTS, b=2),
+                in_=wd_raw[g, d].rearrange("p (m t b) -> p t m b", t=SLOTS, b=2),
             )
 
-        def order_wd_scales(g):
-            src = sraw_first[:] if g == 0 else sraw_rest[:]
+        def order_scale_rows(dst, src):
             nc.vector.tensor_copy(
-                out=(wd_scales[0] if g == 0 else sord_rest)[:].rearrange("p c (t m) -> p c t m", t=4),
-                in_=src.rearrange("p c (m t) -> p c t m", t=4),
+                out=dst[:].rearrange("p d (t m) -> p d t m", t=SLOTS),
+                in_=src[:].rearrange("p d (m t) -> p d t m", t=SLOTS),
             )
 
-        def multiply(g, h, t, j):
-            c = (j + 1) % PASSES if (g, h) == (0, 0) else j
-            if j == 0:
+        def turn_affine():
+            bank = turn_pool.tile([P, W], F32, name="bank", tag="bank")
+            turn_words(bank, 0, affine_rows[:].bitcast(F32))
+            src = bank[:, 0 : 2 * P].bitcast(BF16).rearrange("p (u r e) -> p u r e", u=2, e=2)
+            nc.scalar.activation(
+                out=affine[:].rearrange("p r (u e) -> p u r e", u=2), in_=src[:, :, 0:AFFINE_ROWS, :], func=ACT.Copy
+            )
+
+
+        def multiply(g, h, t, c, order=(SKIP, DEEP_LO, DEEP_HI)):
+            if c == order[0]:
                 acc[g, h, t] = acc_pool.tile([P, W], F32, name="acc%d" % t, tag="acc%d" % t)
             cols = slice(t * P, (t + 1) * P)
-            if c == 0:
+            if c == SKIP:
                 lhs, lhs_scale = ws_codes[:, g, cols].bitcast(FP8X4), ws_scales[:, g, cols]
             else:
-                lhs = wd_words[g][:, c - 1, 2 * P * t : 2 * P * (t + 1)].bitcast(FP4X4)
-                lhs_scale = wd_scales[g][:, c - 1, cols]
+                lhs = wd_words[g][:, c - DEEP_LO, 2 * P * t : 2 * P * (t + 1)].bitcast(FP4X4)
+                lhs_scale = wd_scales[g][:, c - DEEP_LO, cols]
             px = slice(h * W, (h + 1) * W)
             nc.tensor.matmul_mx(
-                out=acc[g, h, t][:], lhsT=lhs, lhsT_scale=lhs_scale,
-                rhs=x_codes[:, c, px].bitcast(FP8X4), rhs_scale=x_scales[:, c, px],
-                start=(j == 0), stop=(j == PASSES - 1),
+                out=acc[g, h, t][:],
+                lhsT=lhs,
+                lhsT_scale=lhs_scale,
+                rhs=x_codes[:, c, px].bitcast(FP8X4),
+                rhs_scale=x_scales[:, c, px],
+                start=(c == order[0]),
+                stop=(c == order[-1]),
             )
 
         def relu_out(g, h, t, px=slice(0, W)):
-            if (g, h) not in act_out:
-                act_out[g, h] = deep3.tile([P, 4, W], F32, name="act_out", tag="act_out")
+            if t == 0:
+                relu[g, h] = triple.tile([P, SLOTS, W], F32, name="relu", tag="relu")
             nc.scalar.activation(
-                out=act_out[g, h][:, t, px], in_=acc[g, h, t][:, px], func=ACT.Relu,
-                bias=affine[:, 8 + g, t : t + 1], scale=affine[:, g, t : t + 1],
+                out=relu[g, h][:, t, px],
+                in_=acc[g, h, t][:, px],
+                func=ACT.Relu,
+                bias=affine[:, SHIFT_ROW + g, t : t + 1],
+                scale=affine[:, g, t : t + 1],
             )
 
         def clamp(out, in_):
             nc.vector.tensor_scalar(out=out, in0=in_, scalar1=CAP, scalar2=0.0, op0=ALU.min, op1=ALU.max)
 
-        def clamp_early(g, h, ts, first_tile):
-            part = act_out[g, h][:, ts, first_tile * P : W]
-            clamp(part, part)
-
         def turn_y(g, h, i, t):
-            if ("y", g, h, i) not in banks:
-                banks["y", g, h, i] = turn_pool.tile([P, W], F32, name="bank", tag="bank")
-            nc.tensor.transpose(banks["y", g, h, i][:, t * P : (t + 1) * P], act_out[g, h][:, t, i * P : (i + 1) * P], ident[:])
+            if t == 0:
+                banks[g, h, i] = turn_pool.tile([P, W], F32, name="bank", tag="bank")
+            nc.tensor.transpose(banks[g, h, i][:, t * P : (t + 1) * P], relu[g, h][:, t, i * P : (i + 1) * P], ident[:])
 
         def empty_y(g, h, i, on_vector):
             if (g, h) not in y_out:
-                y_out[g, h] = deep3.tile([P, 4, W], F32, name="y_out", tag="y_out")
-            dst = y_out[g, h][:, i, :].rearrange("r (p t) -> r p t", t=4)
-            src = banks["y", g, h, i][:].rearrange("r (t p) -> r p t", t=4)
+                y_out[g, h] = triple.tile([P, TILES, W], F32, name="y_out", tag="y_out")
+            dst = y_out[g, h][:, i, :].rearrange("r (p t) -> r p t", t=SLOTS)
+            src = banks[g, h, i][:].rearrange("r (t p) -> r p t", t=SLOTS)
             if on_vector:
                 clamp(dst, src)
             else:
                 nc.scalar.copy(out=dst, in_=src)
 
-        def group_y(g, h):
-            y_bf[g, h] = stage.tile([P, 4 * W], BF16, name="y_bf", tag="y_bf", align_bytes=64)
-            if POOL:
-                cut = POOL * P
-                dst = y_bf[g, h][:].rearrange("p (m t) -> p m t", t=4)
-                src = act_out[g, h][:].rearrange("p t m -> p m t")
-                nc.gpsimd.tensor_scalar(out=dst[:, 0:cut, :], in0=src[:, 0:cut, :], scalar1=CAP, scalar2=0.0, op0=ALU.min, op1=ALU.max)
-            elif TRICK:
-                clamp(
-                    y_bf[g, h][:].rearrange("p (m i t) -> p m t i", i=4, t=4),
-                    act_out[g, h][:].rearrange("p t (m i) -> p m t i", i=4),
-                )
-            else:
-                clamp(y_bf[g, h][:].rearrange("p (m t) -> p m t", t=4), act_out[g, h][:].rearrange("p t m -> p m t"))
-
-        def quantize_y(g, h):
-            y_codes[g, h] = deep3.tile([P, W], U32, name="y_codes", tag="y_codes", align_bytes=64)
-            if h == 0:
-                y_scales[g] = stage.tile([P, PIXELS], U8, name="y_scales", tag="y_scales", align_bytes=64)
-            nc.vector.quantize_mx(
-                out=y_codes[g, h][:].bitcast(FP8X4), scales=y_scales[g][:, h * W : (h + 1) * W], in_=y_bf[g, h][:]
-            )
-
-        def store_y(g, h, i0, n):
+        def store_y(g, h, tiles):
             dst = y_hbm[h * W : (h + 1) * W, g * W : (g + 1) * W].rearrange("(i p) n -> p i n", p=P)
-            nc.sync.dma_start(out=dst[:, i0 : i0 + n, :], in_=y_out[g, h][:, i0 : i0 + n, :])
+            span = slice(tiles[0], tiles[-1] + 1)
+            nc.sync.dma_start(out=dst[:, span, :], in_=y_out[g, h][:, span, :])
 
-        def store_planes(g, h):
-            dst = out_1[g].rearrange("p m t -> p (m t)").bitcast(I32)
-            if h == HALVES - 1:
-                for q in range(4):
-                    nc.sync.dma_start(
-                        out=out_2[g, 4 * q : 4 * q + 4, :].bitcast(I32),
-                        in_=y_scales[g][32 * q : 32 * q + 4, :].bitcast(I32),
-                    )
-            nc.sync.dma_start(out=dst[:, h * W : (h + 1) * W], in_=y_codes[g, h][:].bitcast(I32))
-
-        units = [(g, h) for g in range(GROUPS) for h in range(HALVES)]
-        first_act = 4 - N_ACT
-        nc.vector.memset(sraw_first[:].rearrange("p c n -> p (c n)").bitcast(I32), 0)
-        nc.vector.memset(vec_rows[:].bitcast(I32), 0)
-        nc.vector.memset(sraw_rest[:].rearrange("p c n -> p (c n)").bitcast(I32), 0)
-        for g in range(1, GROUPS):
-            nc.vector.memset(wd_scales[g][:].rearrange("p c n -> p (c n)").bitcast(I32), 0)
-        make_identity(nc, ident[:])
-        nc.gpsimd.dma_start(out=vec_rows[0:GROUPS, :], in_=scale.rearrange("(g n) -> g n", n=W))
-        nc.gpsimd.dma_start(out=vec_rows[8 : 8 + GROUPS, :], in_=shift.rearrange("(g n) -> g n", n=W))
-
-        def turn_affine():
-            banks["affine"] = turn_pool.tile([P, W], F32, name="bank", tag="bank")
-            vec_words = vec_rows[:].bitcast(F32)
-            for u in range(2):
-                nc.tensor.transpose(banks["affine"][:, u * P : (u + 1) * P], vec_words[:, u : 2 * P : 2], ident[:])
-
-        def copy_affine():
-            nc.scalar.activation(
-                out=affine[:].rearrange("p r (u e) -> p u r e", u=2),
-                in_=banks["affine"][:, 0 : 2 * P].bitcast(BF16).rearrange("p (u r e) -> p u r e", u=2, e=2)[:, :, 0:16, :],
-                func=ACT.Copy,
+        def group_y(g, h):
+            y_bf[g, h] = double.tile([P, SLOTS * W], BF16, name="y_bf", tag="y_bf", align_bytes=64)
+            clamp(
+                y_bf[g, h][:].rearrange("p (m i t) -> p m t i", i=4, t=SLOTS),
+                relu[g, h][:].rearrange("p t (m i) -> p m t i", i=4),
             )
 
-        def clamp_last(t):
-            part = act_out[units[-1]][:, t, NV * P : W]
-            clamp(part, part)
+        def quantize_and_store_planes(g, h):
+            y_codes[g, h] = triple.tile([P, W], U32, name="y_codes", tag="y_codes", align_bytes=64)
+            if h == 0:
+                y_scales[g] = double.tile([P, PIXELS], U8, name="y_scales", tag="y_scales", align_bytes=64)
+            px = slice(h * W, (h + 1) * W)
+            nc.vector.quantize_mx(out=y_codes[g, h][:].bitcast(FP8X4), scales=y_scales[g][:, px], in_=y_bf[g, h][:])
+            if h == HALVES - 1:
+                for quad in range(4):
+                    nc.sync.dma_start(
+                        out=out_2[g, 4 * quad : 4 * quad + 4, :].bitcast(I32),
+                        in_=y_scales[g][32 * quad : 32 * quad + 4, :].bitcast(I32),
+                    )
+            words = out_1[g].rearrange("p m t -> p (m t)").bitcast(I32)
+            nc.sync.dma_start(out=words[:, px], in_=y_codes[g, h][:].bitcast(I32))
 
-        def turn_tile(g, h, i):
-            for t in range(4):
-                turn_y(g, h, i, t)
+        nc.vector.memset(scale_rows_first[:].rearrange("p d n -> p (d n)").bitcast(I32), 0)
+        nc.vector.memset(affine_rows[:].bitcast(I32), 0)
+        nc.vector.memset(scale_rows_later[:].rearrange("p d n -> p (d n)").bitcast(I32), 0)
+        for g in range(1, GROUPS):
+            nc.vector.memset(wd_scales[g][:].rearrange("p d n -> p (d n)").bitcast(I32), 0)
+        make_identity(nc, ident[:])
+        nc.gpsimd.dma_start(out=affine_rows[0:GROUPS, :], in_=scale.rearrange("(g n) -> g n", n=W))
+        nc.gpsimd.dma_start(
+            out=affine_rows[SHIFT_ROW : SHIFT_ROW + GROUPS, :], in_=shift.rearrange("(g n) -> g n", n=W)
+        )
 
-        def turn_last(t):
-            for i in range(4):
-                turn_y(GROUPS - 1, HALVES - 1, i, t)
-
-        load_x(x_deep[:, 0:W], 0, 0, 1)
+        for b in range(2):
+            load_x(x_deep[:, 0:W], 0, b, DEEP_LO)
         load_wd_first(0)
         load_scale_rows_first()
-        load_x(x_deep[:, 0:W], 0, 1, 1)
-        load_x(x_deep[:, W : 2 * W], 0, 0, 2)
-        load_x(x_deep[:, W : 2 * W], 0, 1, 2)
+        for b in range(2):
+            load_x(x_deep[:, W : 2 * W], 0, b, DEEP_HI)
         load_wd_first(1)
-        load_x(x_skip, 0, 0, 0)
-        load_x(x_skip, 0, 1, 0)
+        for b in range(2):
+            load_x(x_skip, 0, b, SKIP)
         load_wd(1, 1)
         load_ws(0, 1)
-        load_x(x_skip, 1, 0, 0)
-        load_x(x_skip, 1, 1, 0)
-        load_scale_rows_rest()
-        load_x(x_deep, 1, 0, 1)
-        load_x(x_deep, 1, 1, 1)
+        for b in range(2):
+            load_x(x_skip, 1, b, SKIP)
+        load_scale_rows_later()
+        for b in range(2):
+            load_x(x_deep, 1, b, DEEP_LO)
         load_ws(1, 1)
 
-        def tx(h, c, b, on_vector=False):
-            turn_x(h, c, b)
-            copy_x(h, c, b, on_vector)
+        def first_unit(c, slots):
+            for t in slots:
+                multiply(0, 0, t, c, order=(DEEP_LO, DEEP_HI, SKIP))
 
-        def passes(j, ts):
-            for t in ts:
-                multiply(0, 0, t, j)
-
-        tx(0, 1, 0)
+        turn_x(0, DEEP_LO, 0, by_activation=True)
         order_wd_words(0, 0)
-        order_wd_scales(0)
-        tx(0, 1, 1)
-        quantize_x(0, 1, 0, 1)
-        quantize_x(0, 1, 1, 1)
-        tx(0, 2, 0)
-        passes(0, (0, 1))
-        tx(0, 2, 1)
+        order_scale_rows(wd_scales[0], scale_rows_first)
+        turn_x(0, DEEP_LO, 1, on_vector=True)
+        quantize_x(0, DEEP_LO, 0, 1)
+        quantize_x(0, DEEP_LO, 1, 1)
+        turn_x(0, DEEP_HI, 0)
+        turn_x(0, DEEP_HI, 1)
+        first_unit(DEEP_LO, (0, 1))
         order_wd_words(0, 1)
         order_wd_words(1, 0)
         order_wd_words(1, 1)
-        passes(0, (2, 3))
-        quantize_x(0, 2)
-        tx(0, 0, 0)
-        tx(0, 0, 1)
-        group_ws(0, 0, 3, True)
-        group_ws(0, 3, 1, False)
-        passes(1, (0, 1))
-        quantize_x(0, 0)
-        tx(1, 0, 0)
-        tx(1, 0, 1)
+        quantize_x(0, DEEP_HI)
+        turn_x(0, SKIP, 0)
+        first_unit(DEEP_LO, (2, 3))
+        turn_x(0, SKIP, 1)
+        group_ws(0, 0, 3, on_vector=True)
+        group_ws(0, 3, 1)
+        first_unit(DEEP_HI, (0, 1))
+        quantize_x(0, SKIP)
+        turn_x(1, SKIP, 0)
+        turn_x(1, SKIP, 1)
         quantize_ws(0)
-        order_wd_scales(1)
+        order_scale_rows(scale_rows_ordered, scale_rows_later)
         load_ws(2, 1)
         load_wd(2, 2)
         place_scale_rows(1)
-        passes(1, (2, 3))
-        quantize_x(1, 0)
+        first_unit(DEEP_HI, (2, 3))
+        quantize_x(1, SKIP)
         turn_affine()
-        copy_affine()
-        tx(1, 1, 0, True)
-        tx(1, 1, 1)
-        passes(2, (0, 1))
+        turn_x(1, DEEP_LO, 0, on_vector=True)
+        turn_x(1, DEEP_LO, 1)
+        first_unit(SKIP, (0, 1))
         relu_out(0, 0, 0)
         relu_out(0, 0, 1)
-        quantize_x(1, 1)
-        tx(1, 2, 0, True)
-        tx(1, 2, 1)
-        passes(2, (2, 3))
+        quantize_x(1, DEEP_LO)
+        turn_x(1, DEEP_HI, 0, on_vector=True)
+        turn_x(1, DEEP_HI, 1)
+        first_unit(SKIP, (2, 3))
         relu_out(0, 0, 2)
-        group_ws(1, 0, 2, True)
-        quantize_x(1, 2)
-        group_ws(1, 2, 2, True)
+        group_ws(1, 0, 2, on_vector=True)
+        quantize_x(1, DEEP_HI)
+        group_ws(1, 2, 2, on_vector=True)
         load_ws(3, 1)
         place_scale_rows(2)
         load_wd(4, 2)
@@ -366,81 +342,71 @@ def tile_skip_expand_relu6_g5_kernel(
         place_scale_rows(4)
         place_scale_rows(5)
 
-        def prepare(s, piece):
-            wg = (s + 3) // 2
-            if s % 2 == 1 and wg < GROUPS:
-                order_wd_words(wg, piece)
-            elif s % 2 == 0 and piece == 1 and wg < GROUPS:
-                quantize_ws(wg)
+        def prepare_on_scalar(s, piece):
+            g = (s + 3) // 2
+            if g < GROUPS:
+                group_ws(g, 2 * ((s + 1) % 2) + piece, 1)
 
-        def prepare_act(s, piece):
-            wg = (s + 3) // 2
-            if wg < GROUPS:
-                group_ws(wg, 2 * ((s + 1) % 2) + piece, 1, False)
+        def prepare_on_vector(s, piece):
+            g = (s + 3) // 2
+            if g < GROUPS and s % 2 == 1:
+                order_wd_words(g, piece)
+            elif g < GROUPS and piece == 1:
+                quantize_ws(g)
 
-        tile_order = list(range(first_act, 4)) + list(range(first_act))
+        units = [(g, h) for g in range(GROUPS) for h in range(HALVES)]
+        last_slot = SLOTS - 1
         for s in range(1, len(units)):
             g, h = units[s]
-            pg, ph = units[s - 1]
-            last = s == len(units) - 1
-            k = KLAST if last else (KLATE if s >= 9 else K)
-            relu_out(pg, ph, 3)
-            clamp_early(pg, ph, slice(0, 4), first_act)
+            before = units[s - 1]
+            early = SLOTS_BEFORE_TURN_LAST if s == len(units) - 1 else SLOTS_BEFORE_TURN
+            relu_out(*before, last_slot)
             if s == 1:
                 quantize_ws(1)
-            prepare_act(s, 0)
-            if s == 1:
-                for j in range(PASSES):
-                    for t in range(k):
-                        multiply(g, h, t, j)
-            for t in range(k):
-                for j in range(PASSES if s > 1 else 0):
-                    multiply(g, h, t, j)
+            prepare_on_scalar(s, 0)
+            pairs = [(t, c) for t in range(early) for c in range(PASSES)]
+            for t, c in sorted(pairs, key=lambda tc_pair: tc_pair[1]) if s == 1 else pairs:
+                multiply(g, h, t, c)
+            for t in range(early):
                 relu_out(g, h, t)
-            for i in tile_order:
-                turn_tile(pg, ph, i)
-            for t in range(k, 4):
-                for j in range(PASSES):
-                    multiply(g, h, t, j)
-            prepare(s, 0)
-            group_y(pg, ph)
-            for i in tile_order:
-                empty_y(pg, ph, i, i < first_act)
-            store_y(pg, ph, 2, 2)
-            store_y(pg, ph, 0, 2)
-            if last:
-                for t in range(k):
-                    clamp_last(t)
-            quantize_y(pg, ph)
-            store_planes(pg, ph)
-            for t in range(k, 3):
+            for i in SCALAR_TILES + VECTOR_TILES:
+                for t in range(SLOTS):
+                    turn_y(*before, i, t)
+            for t in range(early, SLOTS):
+                for c in range(PASSES):
+                    multiply(g, h, t, c)
+            group_y(*before)
+            prepare_on_vector(s, 0)
+            for i in SCALAR_TILES + VECTOR_TILES:
+                empty_y(*before, i, i in VECTOR_TILES)
+            store_y(*before, VECTOR_TILES)
+            uncapped = y_out[before][:, SCALAR_TILES[0] : SCALAR_TILES[-1] + 1, :]
+            clamp(uncapped, uncapped)
+            store_y(*before, SCALAR_TILES)
+            quantize_and_store_planes(*before)
+            prepare_on_scalar(s, 1)
+            for t in range(early, last_slot):
                 relu_out(g, h, t)
-                if last:
-                    clamp_last(t)
-            prepare_act(s, 1)
-            prepare(s, 1)
+            prepare_on_vector(s, 1)
 
         g, h = units[-1]
-        relu_out(g, h, 3, slice(0, NV * P))
-        relu_out(g, h, 3, slice(NV * P, W))
-        for i in range(2):
-            for t in range(3):
+
+        def clamp_for_scalar(t):
+            part = relu[g, h][:, t, P:W]
+            clamp(part, part)
+
+        for t in range(last_slot):
+            clamp_for_scalar(t)
+        relu_out(g, h, last_slot, slice(0, P))
+        relu_out(g, h, last_slot, slice(P, W))
+        clamp_for_scalar(last_slot)
+        for t in range(SLOTS):
+            turn_y(g, h, 0, t)
+        for t in range(SLOTS):
+            for i in range(1, TILES):
                 turn_y(g, h, i, t)
-        turn_y(g, h, 0, 3)
-        for i in range(2, 4):
-            for t in range(3):
-                turn_y(g, h, i, t)
-        if TAILV == 0:
-            clamp_last(3)
-        empty_y(g, h, 0, True)
-        if TAILV == 1:
-            clamp_last(3)
-        for i in range(1, 4):
-            turn_y(g, h, i, 3)
-        for i in range(1, 4):
-            empty_y(g, h, i, i < NV)
+        for i in range(TILES):
+            empty_y(g, h, i, i == 0)
+            store_y(g, h, (i,))
         group_y(g, h)
-        quantize_y(g, h)
-        for i in ((0, 1, 2, 3) if NV == 1 else (0, 2, 1, 3)):
-            store_y(g, h, i, 1)
-        store_planes(g, h)
+        quantize_and_store_planes(g, h)

from contextlib import ExitStack

import concourse.mybir as mybir
from concourse.masks import make_identity

F32 = mybir.dt.float32
BF16 = mybir.dt.bfloat16
U32 = mybir.dt.uint32
I32 = mybir.dt.int32
U8 = mybir.dt.uint8
FP8X4 = mybir.dt.float8_e4m3fn_x4
FP4X4 = mybir.dt.float4_e2m1fn_x4
ALU = mybir.AluOpType
ACT = mybir.ActivationFunctionType

PIXELS, C_SKIP, C_DEEP, C_OUT = 1024, 512, 1024, 3072
FLOPS = 2 * PIXELS * (C_SKIP + C_DEEP) * C_OUT
CAP = 6.0

P = 128
W = 512
SLOTS = 4
TILES = W // P
GROUPS = C_OUT // W
HALVES = PIXELS // W
SKIP, DEEP_LO, DEEP_HI = 0, 1, 2
PASSES = 3
SHIFT_ROW = 8
AFFINE_ROWS = 16
VECTOR_TILES, SCALAR_TILES = (0, 1), (2, 3)
SLOTS_BEFORE_TURN, SLOTS_BEFORE_TURN_LAST = 2, 1


def tile_skip_expand_relu6_g5_kernel(
    tc, skip, deep, w_skip, w_deep_words, w_deep_scales, scale, shift, out_0, out_1, out_2
):
    nc = tc.nc
    x_skip = skip.flatten_outer_dims()
    x_deep = deep.flatten_outer_dims()
    y_hbm = out_0.flatten_outer_dims()

    with ExitStack() as ctx:
        keep = ctx.enter_context(tc.tile_pool(name="keep", bufs=1))
        double = ctx.enter_context(tc.tile_pool(name="double", bufs=2))
        triple = ctx.enter_context(tc.tile_pool(name="triple", bufs=3))
        acc_pool = ctx.enter_context(tc.psum_pool(name="acc", bufs=1))
        turn_pool = ctx.enter_context(tc.psum_pool(name="turn", bufs=4))
        ctx.enter_context(tc.manual_schedule())

        ident = keep.tile([P, P], F32, name="ident")
        affine_rows = keep.tile([P, W], BF16, name="affine_rows")
        affine = keep.tile([P, AFFINE_ROWS, SLOTS], F32, name="affine")
        x_codes = keep.tile([P, PASSES, PIXELS], U32, name="x_codes", align_bytes=64)
        x_scales = keep.tile([P, PASSES, PIXELS], U8, name="x_scales", align_bytes=64)
        wd_words, wd_scales = {}, {}
        for g in range(GROUPS):
            wd_words[g] = keep.tile([P, 2, 2 * W], U8, name="wd_words_%d" % g, align_bytes=64)
            wd_scales[g] = keep.tile([P, 2, W], U8, name="wd_scales_%d" % g, align_bytes=64)
        ws_codes = keep.tile([P, GROUPS, W], U32, name="ws_codes", align_bytes=64)
        ws_scales = keep.tile([P, GROUPS, W], U8, name="ws_scales", align_bytes=64)
        scale_rows_first = keep.tile([P, 2, W], U8, name="scale_rows_first")
        scale_rows_later = keep.tile([P, 2, W], U8, name="scale_rows_later")
        scale_rows_ordered = keep.tile([P, 2, W], U8, name="scale_rows_ordered")

        x_raw, ws_raw, wd_raw = {}, {}, {}
        x_grouped, ws_grouped, acc, relu, banks, y_out, y_bf, y_codes, y_scales = {}, {}, {}, {}, {}, {}, {}, {}, {}


        def load_x(src, h, b, first_pass):
            width = src.shape[1]
            raw = keep.tile([P, 2, width], BF16, name="x_raw_%d_%d_%d" % (first_pass, h, b))
            rows = slice(h * W + b * 2 * P, h * W + (b + 1) * 2 * P)
            nc.sync.dma_start(out=raw[:], in_=src[rows, :].rearrange("(p i) k -> p i k", i=2))
            for j in range(width // W):
                x_raw[h, first_pass + j, b] = raw[:, :, j * W : (j + 1) * W]

        def load_ws(g, n):
            cols = slice(g * W, (g + n) * W)
            raw = keep.tile([P, SLOTS, n * W], BF16, name="ws_raw_%d" % g)
            nc.sync.dma_start(out=raw[:], in_=w_skip[:, cols].rearrange("(p j) n -> p j n", j=SLOTS))
            for j in range(n):
                ws_raw[g + j] = raw[:, :, j * W : (j + 1) * W]

        def load_wd(g, n):
            cols = slice(2 * g * W, 2 * (g + n) * W)
            src = w_deep_words[:, :, cols].rearrange("d p b -> p d b")
            raw = keep.tile([P, 2, 2 * n * W], U8, name="wd_raw_%d" % g)
            nc.sync.dma_start(out=raw[:].bitcast(I32), in_=src.bitcast(I32))
            for j in range(n):
                for d in range(2):
                    wd_raw[g + j, d] = raw[:, d, 2 * j * W : 2 * (j + 1) * W]

        def load_wd_first(d):
            raw = keep.tile([P, 2 * W], U8, name="wd_raw_first_%d" % d)
            nc.sync.dma_start(out=raw[:].bitcast(I32), in_=w_deep_words[d, :, 0 : 2 * W].bitcast(I32))
            wd_raw[0, d] = raw[:]

        def load_scale_rows_first():
            for quad in range(4):
                src = w_deep_scales[:, 4 * quad : 4 * quad + 4, 0:W].rearrange("d r n -> r d n")
                dst = scale_rows_first[32 * quad : 32 * quad + 4, :, :]
                nc.sync.dma_start(out=dst.bitcast(I32), in_=src.bitcast(I32))

        def load_scale_rows_later():
            for g in range(1, GROUPS):
                src = w_deep_scales[:, :, g * W : (g + 1) * W].rearrange("d q n -> q d n")
                dst = scale_rows_later[16 * g : 16 * g + 16, :, :]
                nc.sync.dma_start(out=dst.bitcast(I32), in_=src.bitcast(I32))

        def place_scale_rows(g):
            for quad in range(4):
                first = 16 * g + 4 * quad
                src = scale_rows_ordered[first : first + 4, :, :].rearrange("r d n -> r (d n)")
                dst = wd_scales[g][32 * quad : 32 * quad + 4, :, :].rearrange("r d n -> r (d n)")
                nc.sync.dma_start(out=dst.bitcast(I32), in_=src.bitcast(I32))


        def turn_words(bank, first, words):
            for u in range(2):
                nc.tensor.transpose(bank[:, (first + u) * P : (first + u + 1) * P], words[:, u : 2 * P : 2], ident[:])

        def turn_x(h, c, b, on_vector=False, by_activation=False):
            bank = turn_pool.tile([P, W], F32, name="bank", tag="bank")
            for i in range(2):
                turn_words(bank, 2 * i, x_raw[h, c, b][:, i, :].bitcast(F32))
            if b == 0:
                x_grouped[h, c] = triple.tile([P, SLOTS * W], BF16, name="x_grouped", tag="x_grouped", align_bytes=64)
            part = x_grouped[h, c][:, b * 2 * W : (b + 1) * 2 * W]
            if by_activation:
                nc.scalar.activation(
                    out=part.rearrange("p (r j e) -> p r j e", j=4, e=2),
                    in_=bank[:].bitcast(BF16).rearrange("p (j r e) -> p r j e", j=4, e=2),
                    func=ACT.Copy,
                )
                return
            dst = part.bitcast(F32).rearrange("p (r j) -> p r j", j=4)
            src = bank[:].rearrange("p (j r) -> p r j", j=4)
            if on_vector:
                nc.vector.tensor_copy(out=dst, in_=src)
            else:
                nc.scalar.copy(out=dst, in_=src)

        def quantize_x(h, c, b0=0, n=2):
            cols = slice(h * W + b0 * 2 * P, h * W + (b0 + n) * 2 * P)
            nc.vector.quantize_mx(
                out=x_codes[:, c, cols].bitcast(FP8X4),
                scales=x_scales[:, c, cols],
                in_=x_grouped[h, c][:, b0 * 2 * W : (b0 + n) * 2 * W],
            )

        def group_ws(g, t, n, on_vector=False):
            if t == 0:
                ws_grouped[g] = double.tile([P, SLOTS * W], BF16, name="ws_grouped", tag="ws_grouped", align_bytes=64)
            dst = ws_grouped[g][:].rearrange("p (t m j) -> p t m j", t=SLOTS, j=SLOTS)[:, t : t + n, :, :]
            src = ws_raw[g].rearrange("p j (m t) -> p t m j", t=SLOTS)[:, t : t + n, :, :]
            if on_vector:
                nc.vector.tensor_copy(out=dst, in_=src)
            else:
                nc.scalar.copy(out=dst, in_=src)

        def quantize_ws(g):
            nc.vector.quantize_mx(out=ws_codes[:, g, :].bitcast(FP8X4), scales=ws_scales[:, g, :], in_=ws_grouped[g][:])

        def order_wd_words(g, d):
            nc.vector.tensor_copy(
                out=wd_words[g][:, d, :].rearrange("p (t m b) -> p t m b", t=SLOTS, b=2),
                in_=wd_raw[g, d].rearrange("p (m t b) -> p t m b", t=SLOTS, b=2),
            )

        def order_scale_rows(dst, src):
            nc.vector.tensor_copy(
                out=dst[:].rearrange("p d (t m) -> p d t m", t=SLOTS),
                in_=src[:].rearrange("p d (m t) -> p d t m", t=SLOTS),
            )

        def turn_affine():
            bank = turn_pool.tile([P, W], F32, name="bank", tag="bank")
            turn_words(bank, 0, affine_rows[:].bitcast(F32))
            src = bank[:, 0 : 2 * P].bitcast(BF16).rearrange("p (u r e) -> p u r e", u=2, e=2)
            nc.scalar.activation(
                out=affine[:].rearrange("p r (u e) -> p u r e", u=2), in_=src[:, :, 0:AFFINE_ROWS, :], func=ACT.Copy
            )


        def multiply(g, h, t, c, order=(SKIP, DEEP_LO, DEEP_HI)):
            if c == order[0]:
                acc[g, h, t] = acc_pool.tile([P, W], F32, name="acc%d" % t, tag="acc%d" % t)
            cols = slice(t * P, (t + 1) * P)
            if c == SKIP:
                lhs, lhs_scale = ws_codes[:, g, cols].bitcast(FP8X4), ws_scales[:, g, cols]
            else:
                lhs = wd_words[g][:, c - DEEP_LO, 2 * P * t : 2 * P * (t + 1)].bitcast(FP4X4)
                lhs_scale = wd_scales[g][:, c - DEEP_LO, cols]
            px = slice(h * W, (h + 1) * W)
            nc.tensor.matmul_mx(
                out=acc[g, h, t][:],
                lhsT=lhs,
                lhsT_scale=lhs_scale,
                rhs=x_codes[:, c, px].bitcast(FP8X4),
                rhs_scale=x_scales[:, c, px],
                start=(c == order[0]),
                stop=(c == order[-1]),
            )

        def relu_out(g, h, t, px=slice(0, W)):
            if t == 0:
                relu[g, h] = triple.tile([P, SLOTS, W], F32, name="relu", tag="relu")
            nc.scalar.activation(
                out=relu[g, h][:, t, px],
                in_=acc[g, h, t][:, px],
                func=ACT.Relu,
                bias=affine[:, SHIFT_ROW + g, t : t + 1],
                scale=affine[:, g, t : t + 1],
            )

        def clamp(out, in_):
            nc.vector.tensor_scalar(out=out, in0=in_, scalar1=CAP, scalar2=0.0, op0=ALU.min, op1=ALU.max)

        def turn_y(g, h, i, t):
            if t == 0:
                banks[g, h, i] = turn_pool.tile([P, W], F32, name="bank", tag="bank")
            nc.tensor.transpose(banks[g, h, i][:, t * P : (t + 1) * P], relu[g, h][:, t, i * P : (i + 1) * P], ident[:])

        def empty_y(g, h, i, on_vector):
            if (g, h) not in y_out:
                y_out[g, h] = triple.tile([P, TILES, W], F32, name="y_out", tag="y_out")
            dst = y_out[g, h][:, i, :].rearrange("r (p t) -> r p t", t=SLOTS)
            src = banks[g, h, i][:].rearrange("r (t p) -> r p t", t=SLOTS)
            if on_vector:
                clamp(dst, src)
            else:
                nc.scalar.copy(out=dst, in_=src)

        def store_y(g, h, tiles):
            dst = y_hbm[h * W : (h + 1) * W, g * W : (g + 1) * W].rearrange("(i p) n -> p i n", p=P)
            span = slice(tiles[0], tiles[-1] + 1)
            nc.sync.dma_start(out=dst[:, span, :], in_=y_out[g, h][:, span, :])

        def group_y(g, h):
            y_bf[g, h] = double.tile([P, SLOTS * W], BF16, name="y_bf", tag="y_bf", align_bytes=64)
            clamp(
                y_bf[g, h][:].rearrange("p (m i t) -> p m t i", i=4, t=SLOTS),
                relu[g, h][:].rearrange("p t (m i) -> p m t i", i=4),
            )

        def quantize_and_store_planes(g, h):
            y_codes[g, h] = triple.tile([P, W], U32, name="y_codes", tag="y_codes", align_bytes=64)
            if h == 0:
                y_scales[g] = double.tile([P, PIXELS], U8, name="y_scales", tag="y_scales", align_bytes=64)
            px = slice(h * W, (h + 1) * W)
            nc.vector.quantize_mx(out=y_codes[g, h][:].bitcast(FP8X4), scales=y_scales[g][:, px], in_=y_bf[g, h][:])
            if h == HALVES - 1:
                for quad in range(4):
                    nc.sync.dma_start(
                        out=out_2[g, 4 * quad : 4 * quad + 4, :].bitcast(I32),
                        in_=y_scales[g][32 * quad : 32 * quad + 4, :].bitcast(I32),
                    )
            words = out_1[g].rearrange("p m t -> p (m t)").bitcast(I32)
            nc.sync.dma_start(out=words[:, px], in_=y_codes[g, h][:].bitcast(I32))

        nc.vector.memset(scale_rows_first[:].rearrange("p d n -> p (d n)").bitcast(I32), 0)
        nc.vector.memset(affine_rows[:].bitcast(I32), 0)
        nc.vector.memset(scale_rows_later[:].rearrange("p d n -> p (d n)").bitcast(I32), 0)
        for g in range(1, GROUPS):
            nc.vector.memset(wd_scales[g][:].rearrange("p d n -> p (d n)").bitcast(I32), 0)
        make_identity(nc, ident[:])
        nc.gpsimd.dma_start(out=affine_rows[0:GROUPS, :], in_=scale.rearrange("(g n) -> g n", n=W))
        nc.gpsimd.dma_start(
            out=affine_rows[SHIFT_ROW : SHIFT_ROW + GROUPS, :], in_=shift.rearrange("(g n) -> g n", n=W)
        )

        for b in range(2):
            load_x(x_deep[:, 0:W], 0, b, DEEP_LO)
        load_wd_first(0)
        load_scale_rows_first()
        for b in range(2):
            load_x(x_deep[:, W : 2 * W], 0, b, DEEP_HI)
        load_wd_first(1)
        for b in range(2):
            load_x(x_skip, 0, b, SKIP)
        load_wd(1, 1)
        load_ws(0, 1)
        for b in range(2):
            load_x(x_skip, 1, b, SKIP)
        load_scale_rows_later()
        for b in range(2):
            load_x(x_deep, 1, b, DEEP_LO)
        load_ws(1, 1)

        def first_unit(c, slots):
            for t in slots:
                multiply(0, 0, t, c, order=(DEEP_LO, DEEP_HI, SKIP))

        turn_x(0, DEEP_LO, 0, by_activation=True)
        order_wd_words(0, 0)
        order_scale_rows(wd_scales[0], scale_rows_first)
        turn_x(0, DEEP_LO, 1, on_vector=True)
        quantize_x(0, DEEP_LO, 0, 1)
        quantize_x(0, DEEP_LO, 1, 1)
        turn_x(0, DEEP_HI, 0)
        turn_x(0, DEEP_HI, 1)
        first_unit(DEEP_LO, (0, 1))
        order_wd_words(0, 1)
        order_wd_words(1, 0)
        order_wd_words(1, 1)
        quantize_x(0, DEEP_HI)
        turn_x(0, SKIP, 0)
        first_unit(DEEP_LO, (2, 3))
        turn_x(0, SKIP, 1)
        group_ws(0, 0, 3, on_vector=True)
        group_ws(0, 3, 1)
        first_unit(DEEP_HI, (0, 1))
        quantize_x(0, SKIP)
        turn_x(1, SKIP, 0)
        turn_x(1, SKIP, 1)
        quantize_ws(0)
        order_scale_rows(scale_rows_ordered, scale_rows_later)
        load_ws(2, 1)
        load_wd(2, 2)
        place_scale_rows(1)
        first_unit(DEEP_HI, (2, 3))
        quantize_x(1, SKIP)
        turn_affine()
        turn_x(1, DEEP_LO, 0, on_vector=True)
        turn_x(1, DEEP_LO, 1)
        first_unit(SKIP, (0, 1))
        relu_out(0, 0, 0)
        relu_out(0, 0, 1)
        quantize_x(1, DEEP_LO)
        turn_x(1, DEEP_HI, 0, on_vector=True)
        turn_x(1, DEEP_HI, 1)
        first_unit(SKIP, (2, 3))
        relu_out(0, 0, 2)
        group_ws(1, 0, 2, on_vector=True)
        quantize_x(1, DEEP_HI)
        group_ws(1, 2, 2, on_vector=True)
        load_ws(3, 1)
        place_scale_rows(2)
        load_wd(4, 2)
        place_scale_rows(3)
        load_ws(4, 2)
        place_scale_rows(4)
        place_scale_rows(5)

        def prepare_on_scalar(s, piece):
            g = (s + 3) // 2
            if g < GROUPS:
                group_ws(g, 2 * ((s + 1) % 2) + piece, 1)

        def prepare_on_vector(s, piece):
            g = (s + 3) // 2
            if g < GROUPS and s % 2 == 1:
                order_wd_words(g, piece)
            elif g < GROUPS and piece == 1:
                quantize_ws(g)

        units = [(g, h) for g in range(GROUPS) for h in range(HALVES)]
        last_slot = SLOTS - 1
        for s in range(1, len(units)):
            g, h = units[s]
            before = units[s - 1]
            early = SLOTS_BEFORE_TURN_LAST if s == len(units) - 1 else SLOTS_BEFORE_TURN
            relu_out(*before, last_slot)
            if s == 1:
                quantize_ws(1)
            prepare_on_scalar(s, 0)
            pairs = [(t, c) for t in range(early) for c in range(PASSES)]
            for t, c in sorted(pairs, key=lambda tc_pair: tc_pair[1]) if s == 1 else pairs:
                multiply(g, h, t, c)
            for t in range(early):
                relu_out(g, h, t)
            for i in SCALAR_TILES + VECTOR_TILES:
                for t in range(SLOTS):
                    turn_y(*before, i, t)
            for t in range(early, SLOTS):
                for c in range(PASSES):
                    multiply(g, h, t, c)
            group_y(*before)
            prepare_on_vector(s, 0)
            for i in SCALAR_TILES + VECTOR_TILES:
                empty_y(*before, i, i in VECTOR_TILES)
            store_y(*before, VECTOR_TILES)
            uncapped = y_out[before][:, SCALAR_TILES[0] : SCALAR_TILES[-1] + 1, :]
            clamp(uncapped, uncapped)
            store_y(*before, SCALAR_TILES)
            quantize_and_store_planes(*before)
            prepare_on_scalar(s, 1)
            for t in range(early, last_slot):
                relu_out(g, h, t)
            prepare_on_vector(s, 1)

        g, h = units[-1]

        def clamp_for_scalar(t):
            part = relu[g, h][:, t, P:W]
            clamp(part, part)

        for t in range(last_slot):
            clamp_for_scalar(t)
        relu_out(g, h, last_slot, slice(0, P))
        relu_out(g, h, last_slot, slice(P, W))
        clamp_for_scalar(last_slot)
        for t in range(SLOTS):
            turn_y(g, h, 0, t)
        for t in range(SLOTS):
            for i in range(1, TILES):
                turn_y(g, h, i, t)
        for i in range(TILES):
            empty_y(g, h, i, i == 0)
            store_y(g, h, (i,))
        group_y(g, h)
        quantize_and_store_planes(g, h)
